import numpy as np
import ml_dtypes


def mxq(x, axis, fmt="e4m3"):
    dtype, down = {"e4m3": (ml_dtypes.float8_e4m3fn, 7), "e5m2": (ml_dtypes.float8_e5m2, 14)}[fmt]
    v = np.moveaxis(np.asarray(x, np.float32).astype(ml_dtypes.bfloat16).astype(np.float64), axis, -1)
    blocks = v.reshape(v.shape[:-1] + (-1, 32))
    amax = np.abs(blocks).max(-1, keepdims=True)
    byte = np.maximum(np.where(amax > 0, np.frexp(amax)[1] - 1 + 127, 0) - down, 1)
    scale = np.exp2(byte - 127.0)
    codes = (blocks / scale).astype(np.float32).astype(dtype).astype(np.float64)
    return np.moveaxis((codes * scale).reshape(v.shape), -1, axis)


WIDE = False


def mx_kscale(k):
    if not WIDE:
        return np.ones(k)
    levels = np.array([10, -10, 5, -5, 0])
    if k % 512:
        return np.exp2(np.random.permutation(np.resize(levels, k // 32))).repeat(32)
    a = np.empty((k // 512, 16))
    for p in range(k // 512):
        a[p, :8] = np.random.permutation(np.resize(levels, 8))
        for g in range(8):
            far = levels[np.abs(levels - a[p, g]) >= 10]
            a[p, g + 8] = far[np.random.randint(len(far))]
    return np.exp2(a.ravel()).repeat(32)


BF16 = ml_dtypes.bfloat16


def bf(x):
    return np.asarray(x, np.float32).astype(BF16)


def f64(x):
    return np.asarray(x).astype(np.float64)


E2M1 = np.array([0.0, 0.5, 1.0, 1.5, 2.0, 3.0, 4.0, 6.0, -0.0, -0.5, -1.0, -1.5, -2.0, -3.0, -4.0, -6.0])


def pack_weight(w, fmt):
    k, n = w.shape
    w = f64(bf(w)).reshape(k // 32, 32, n)
    amax = np.abs(w).max(1)
    if fmt == "e4m3":
        byte = np.frexp(amax)[1] - 1 + 127 - 7
    else:
        mant, ex = np.frexp(amax / 6.0)
        byte = np.where(mant > 0.5, ex, ex - 1) + 127
    byte = np.clip(np.where(amax > 0, byte, 1), 1, 254)
    scaled = (w * np.exp2(127.0 - byte)[:, None, :]).reshape(k, n).astype(np.float32)
    by_word = np.ascontiguousarray(scaled.reshape(k // 512, 128, 4, n).transpose(0, 1, 3, 2))
    if fmt == "e4m3":
        words = by_word.astype(ml_dtypes.float8_e4m3fn).view(np.uint8)
    else:
        c = by_word.astype(ml_dtypes.float4_e2m1fn).view(np.uint8) & 0xF
        words = c[..., 0::2] | (c[..., 1::2] << 4)
    return np.ascontiguousarray(words), np.ascontiguousarray(byte.astype(np.uint8).reshape(k // 512, 16, n))


def unpack_weight(words, scales, fmt):
    g, p, n, _ = words.shape
    if fmt == "e4m3":
        vals = np.ascontiguousarray(words).view(ml_dtypes.float8_e4m3fn).astype(np.float64)
    else:
        nib = np.empty((g, p, n, 4), np.uint8)
        nib[..., 0::2] = words & 0xF
        nib[..., 1::2] = words >> 4
        vals = E2M1[nib]
    vals = vals * np.repeat(np.exp2(scales.astype(np.float64) - 127.0), 8, axis=1)[..., None]
    return vals.transpose(0, 1, 3, 2).reshape(g * 512, n)
def pack4(w):
    words, scales = pack_weight(w, "e2m1")
    return words.reshape(words.shape[0], 128, -1), scales


def unpack4(words, scales):
    return unpack_weight(words.reshape(words.shape[0], 128, -1, 2), scales, "e2m1")


def planes(Y):
    n, m = Y.shape
    b = f64(bf(Y)).reshape(n // 32, 32, m)
    amax = np.abs(b).max(1)
    byte = np.clip(np.where(amax > 0, np.frexp(amax)[1] - 1 + 127 - 7, 1), 1, 254)
    codes = (b * np.exp2(127.0 - byte)[:, None, :]).reshape(n, m).astype(np.float32).astype(ml_dtypes.float8_e4m3fn).view(np.uint8)
    words = codes.reshape(n // 512, 128, 4, m).transpose(0, 1, 3, 2)
    return np.ascontiguousarray(words), np.ascontiguousarray(byte.astype(np.uint8).reshape(n // 512, 16, m))


M, D, F, N = 768, 1024, 2048, 1536


def setup_inputs():
    sd = mx_kscale(D)
    sf = mx_kscale(F)
    X = np.random.randn(D, M) * sd[:, None]
    W1 = np.random.randn(D, F) / np.sqrt(D) * sf[None, :] / sd[:, None]
    W2 = 2.0 * np.random.randn(F, N) / np.sqrt(F) / sf[:, None]
    x_words, x_scales = pack_weight(X, "e4m3")
    w1_words, w1_scales = pack4(W1)
    z = 1.5 * np.random.randn(M, F)
    log_rate = 0.8 * np.random.randn(N)[None, :] + 0.3 * np.random.randn(M, N)
    exposure = np.exp(0.3 * np.random.randn(M))
    return {"x_words": x_words, "x_scales": x_scales, "w1_words": w1_words, "w1_scales": w1_scales,
            "z": bf(z), "w2": bf(W2), "log_rate": bf(log_rate), "exposure": bf(exposure)}


def reference(x_words, x_scales, w1_words, w1_scales, z, w2, log_rate, exposure):
    X = unpack_weight(x_words, x_scales, "e4m3")
    W1 = unpack4(w1_words, w1_scales)
    U = X.T @ W1
    H = U * (1.0 / (1.0 + np.exp(-f64(z))))
    R = mxq(H, 1, "e4m3") @ mxq(f64(w2), 0, "e4m3")
    y = R * np.exp(f64(log_rate)) * f64(exposure)[:, None]
    Y = y.T
    words, scales = planes(Y)
    return y, words, scales

@@ -1,0 +1,350 @@
+from contextlib import ExitStack
+
+import concourse.mybir as mybir
+from concourse.masks import make_identity
+
+M, D, F, N = 768, 1024, 2048, 1536
+FLOPS = 2 * M * D * F + 2 * M * F * N
+
+F32 = mybir.dt.float32
+BF16 = mybir.dt.bfloat16
+I32 = mybir.dt.int32
+U32 = mybir.dt.uint32
+U8 = mybir.dt.uint8
+FP8X4 = mybir.dt.float8_e4m3fn_x4
+FP4X4 = mybir.dt.float4_e2m1fn_x4
+ACT = mybir.ActivationFunctionType
+ALU = mybir.AluOpType
+
+P = 128
+G = 512
+MT = M // P
+DG = D // G
+FG = F // G
+NG = N // G
+
+W2_PLAN = [(1, 160, 0), (2, 160, 0), (3, 160, 0), (4, 160, 0), (5, 224, 0), (6, 224, 0), (8, 224, 0), (9, 224, 0), (10, 288, 0), (12, 288, 0), (13, 288, 0), (15, 288, 0)]
+CAST = "v" * 18
+IL4 = True
+
+
+def tile_curvature_scaled_tangents_h2_kernel(
+    tc, x_words, x_scales, w1_words, w1_scales, z, w2, log_rate, exposure, out_0, out_1, out_2
+):
+    nc = tc.nc
+    with ExitStack() as ctx:
+        keep = ctx.enter_context(tc.tile_pool(name="keep", bufs=1))
+        flow = ctx.enter_context(tc.tile_pool(name="flow", bufs=2))
+        psum = ctx.enter_context(tc.psum_pool(name="psum", bufs=1))
+        ctx.enter_context(tc.manual_schedule())
+
+        x_plane = keep.tile([P, DG, M], U8, align_bytes=64)
+        w1_plane = keep.tile([P, DG, F], U8, align_bytes=64)
+        x_first = keep.tile([P, DG, 2 * P], U32, align_bytes=64)
+        x_rest = keep.tile([P, DG, M - 2 * P], U32, align_bytes=64)
+        w1_half = [keep.tile([P, DG, F], U8, align_bytes=64, name="w1_half%d" % h) for h in range(2)]
+        ident = keep.tile([P, P], F32, align_bytes=64)
+        expo_rows = keep.tile([P, P], BF16, align_bytes=64)
+        expo_rows32 = keep.tile([P, P], F32, align_bytes=64)
+        expo = keep.tile([P, 8], F32, align_bytes=64)
+        w2_first = [keep.tile([P, 4, G], BF16, align_bytes=64, name="w2_first%d" % g) for g in range(FG)]
+        w2_rest = [keep.tile([P, 4, N - G], BF16, align_bytes=64, name="w2_rest%d" % g) for g in range(FG)]
+        w2_codes = [keep.tile([P, G], U32, align_bytes=64, name="w2_codes%d" % c) for c in range(NG * FG)]
+        w2_plane = [keep.tile([P, G], U8, align_bytes=64, name="w2_plane%d" % c) for c in range(NG * FG)]
+        h_codes = [keep.tile([P, FG * P], U32, align_bytes=64, name="h_codes%d" % m) for m in range(MT)]
+        h_plane = [keep.tile([P, FG * P], U8, align_bytes=64, name="h_plane%d" % m) for m in range(MT)]
+        y_codes = [keep.tile([P, M], U32, align_bytes=64, name="y_codes%d" % n) for n in range(NG)]
+        y_plane = keep.tile([P, NG, M], U8, align_bytes=64)
+
+        rows, lrs, sig, acc, h_bf, h_tr, h_t, w2_il, curv, y32, y_bf, y_tr, y_t = (
+            {}, {}, {}, {}, {}, {}, {}, {}, {}, {}, {}, {}, {})
+
+        x_view = x_words.rearrange("g p m t -> p g (m t)")
+        w1_view = w1_words.rearrange("g p b -> p g b")
+
+        def load_z(m, halves=1):
+            rows[m] = flow.tile([P, F], BF16, tag="rows", bufs=MT, align_bytes=64, name="z%d" % m)
+            w = F // halves
+            return [
+                (lambda h=h: nc.sync.dma_start(out=rows[m][:, h * w:(h + 1) * w], in_=z[m * P:(m + 1) * P, h * w:(h + 1) * w]))
+                for h in range(halves)
+            ]
+
+        def load_lr(m):
+            lrs[m] = flow.tile([P, N], BF16, tag="rows", bufs=MT, align_bytes=64, name="lr%d" % m)
+            nc.sync.dma_start(out=lrs[m][:], in_=log_rate[m * P:(m + 1) * P, :])
+
+        def load_w2(tile, g, lo, hi):
+            nc.sync.dma_start(out=tile[:], in_=w2[g * G:(g + 1) * G, lo:hi].rearrange("(p j) n -> p j n", j=4))
+
+        def load_plane(queue, plane, scales):
+            for q in range(4):
+                queue.dma_start(
+                    out=plane[32 * q:32 * q + 4, :, :].bitcast(I32),
+                    in_=scales[:, 4 * q:4 * q + 4, :].rearrange("g r n -> r g n").bitcast(I32),
+                )
+
+        def sigmoid(m):
+            for g in range(FG):
+                sig[m, g] = flow.tile([P, G], F32, tag="sig", bufs=2 * FG, align_bytes=64, name="sig")
+                nc.scalar.activation(
+                    out=sig[m, g][:].rearrange("m (u p e) -> m u p e", u=2, e=2),
+                    in_=rows[m][:, g * G:(g + 1) * G].rearrange("m (p u e) -> m u p e", u=2, e=2),
+                    func=ACT.Sigmoid,
+                )
+
+        def stage1_mm(m, g):
+            xt, lo = (x_first, m * P) if m < 2 else (x_rest, (m - 2) * P)
+            acc[m, g] = psum.tile([P, G], F32, tag="acc", bufs=5, name="acc")
+            for d in range(DG):
+                nc.tensor.matmul_mx(
+                    out=acc[m, g][:],
+                    lhsT=xt[:, d, lo:lo + P].bitcast(FP8X4),
+                    lhsT_scale=x_plane[:, d, m * P:(m + 1) * P],
+                    rhs=w1_half[g // 2][:, d, (g % 2) * 2 * G:(g % 2 + 1) * 2 * G].bitcast(FP4X4),
+                    rhs_scale=w1_plane[:, d, g * G:(g + 1) * G],
+                    start=(d == 0),
+                    stop=(d == DG - 1),
+                )
+
+        def stage1_mult(m, g):
+            if g == 0:
+                h_bf[m] = flow.tile([P, F], BF16, tag="h_bf", bufs=2, align_bytes=64, name="h_bf")
+            nc.vector.tensor_tensor(
+                out=h_bf[m][:, g * G:(g + 1) * G].rearrange("m (u p e) -> m u p e", u=2, e=2),
+                in0=acc[m, g][:].rearrange("m (p u e) -> m u p e", u=2, e=2),
+                in1=sig[m, g][:].rearrange("m (u p e) -> m u p e", u=2, e=2),
+                op=ALU.mult,
+            )
+
+        def turn(src_words):
+            bank = psum.tile([P, G], F32, tag="turn", bufs=3, name="turn")
+            k = len(src_words)
+            for s in range(k):
+                nc.tensor.transpose(bank[:, s * P:(s + 1) * P], src_words[s], ident[:])
+            return bank
+
+        def unturn(dst_words, bank, k):
+            nc.scalar.copy(
+                out=dst_words.rearrange("p (a m u) -> p a m u", a=k // 2, u=2),
+                in_=bank[:, 0:k * P].rearrange("p (a u m) -> p a m u", a=k // 2, u=2),
+            )
+
+        def h_turn(m):
+            words = h_bf[m][:].bitcast(F32)
+            h_tr[m] = [turn([words[:, (4 * b + s) * P:(4 * b + s + 1) * P] for s in range(4)]) for b in range(2)]
+
+        def h_unturn(m):
+            h_t[m] = flow.tile([P, F // 2], F32, tag="h_t", bufs=2, align_bytes=64, name="h_t")
+            for b in range(2):
+                unturn(h_t[m][:, b * G:(b + 1) * G], h_tr[m][b], 4)
+
+        def h_quant(m):
+            nc.vector.quantize_mx(out=h_codes[m][:].bitcast(FP8X4), scales=h_plane[m][:], in_=h_t[m][:].bitcast(BF16))
+
+        def w2_views(c, lo, hi):
+            n, g = divmod(c, FG)
+            src = w2_first[g][:, :, lo:hi] if n == 0 else w2_rest[g][:, :, (n - 1) * G + lo:(n - 1) * G + hi]
+            dst = w2_il[c][:, 4 * lo:4 * hi]
+            if IL4:
+                return dst.rearrange("p (c i t) -> p c t i", i=4, t=4), src.rearrange("p t (c i) -> p c t i", i=4)
+            return dst.rearrange("p (c t) -> p c t", t=4), src.rearrange("p t c -> p c t")
+
+        def w2_alloc(c):
+            w2_il[c] = flow.tile([P, 4 * G], BF16, tag="w2_il", bufs=3, align_bytes=64, name="w2_il")
+
+        def w2_vector(c):
+            lo = W2_PLAN[c][1] + W2_PLAN[c][2]
+            if lo < G:
+                dst, src = w2_views(c, lo, G)
+                nc.vector.tensor_copy(out=dst, in_=src)
+
+        def w2_scalar(c):
+            if W2_PLAN[c][1] > 0:
+                dst, src = w2_views(c, 0, W2_PLAN[c][1])
+                nc.scalar.copy(out=dst, in_=src)
+
+        def w2_gpsimd(c):
+            if W2_PLAN[c][2] > 0:
+                dst, src = w2_views(c, W2_PLAN[c][1], W2_PLAN[c][1] + W2_PLAN[c][2])
+                nc.gpsimd.tensor_scalar(out=dst, in0=src, scalar1=1.0, scalar2=-0.0, op0=ALU.mult, op1=ALU.add)
+
+        def w2_quant(c):
+            nc.vector.quantize_mx(out=w2_codes[c][:].bitcast(FP8X4), scales=w2_plane[c][:], in_=w2_il[c][:])
+
+        def curvature(i):
+            n, m = divmod(i, MT)
+            curv[i] = flow.tile([P, G], F32, tag="curv", bufs=4, align_bytes=64, name="curv")
+            nc.scalar.activation(out=curv[i][:], in_=lrs[m][:, n * G:(n + 1) * G], func=ACT.Exp)
+
+        def stage2_mm(i):
+            n, m = divmod(i, MT)
+            acc[i] = psum.tile([P, G], F32, tag="acc", bufs=5, name="acc")
+            for g in range(FG):
+                nc.tensor.matmul_mx(
+                    out=acc[i][:],
+                    lhsT=h_codes[m][:, g * P:(g + 1) * P].bitcast(FP8X4),
+                    lhsT_scale=h_plane[m][:, g * P:(g + 1) * P],
+                    rhs=w2_codes[n * FG + g][:].bitcast(FP8X4),
+                    rhs_scale=w2_plane[n * FG + g][:],
+                    start=(g == 0),
+                    stop=(g == FG - 1),
+                )
+
+        def stage2_mult(i):
+            n, m = divmod(i, MT)
+            y32[i] = flow.tile([P, G], F32, tag="y32", bufs=6, align_bytes=64, name="y32")
+            nc.vector.scalar_tensor_tensor(
+                out=y32[i][:], in0=acc[i][:], scalar=expo[:, m:m + 1], in1=curv[i][:], op0=ALU.mult, op1=ALU.mult
+            )
+            nc.sync.dma_start(out=out_0[m * P:(m + 1) * P, n * G:(n + 1) * G], in_=y32[i][:])
+
+        def y_round(i):
+            y_bf[i] = flow.tile([P, G], BF16, tag="y_bf", bufs=4, align_bytes=64, name="y_bf")
+            dst = y_bf[i][:].rearrange("m (u p e) -> m u p e", u=2, e=2)
+            src = y32[i][:].rearrange("m (p u e) -> m u p e", u=2, e=2)
+            if CAST[i] == "v":
+                nc.vector.tensor_copy(out=dst, in_=src)
+            elif CAST[i] == "s":
+                nc.scalar.copy(out=dst, in_=src)
+            else:
+                nc.gpsimd.tensor_scalar(out=dst, in0=src, scalar1=1.0, scalar2=-0.0, op0=ALU.mult, op1=ALU.add)
+
+        def y_turn(group):
+            src = []
+            for i in group:
+                words = y_bf[i][:].bitcast(F32)
+                src.extend([words[:, 0:P], words[:, P:2 * P]])
+            y_tr[group] = turn(src)
+
+        def y_unturn(group):
+            k = 2 * len(group)
+            y_t[group] = flow.tile([P, k * P], F32, tag="y_t", bufs=2, align_bytes=64, name="y_t")
+            unturn(y_t[group][:], y_tr[group], k)
+
+        def y_quant(group):
+            n, m = divmod(group[0], MT)
+            cols = slice(m * P, (m + len(group)) * P)
+            nc.vector.quantize_mx(
+                out=y_codes[n][:, cols].bitcast(FP8X4), scales=y_plane[:, n, cols], in_=y_t[group][:].bitcast(BF16)
+            )
+
+        def store_codes(n, lo, hi, queue):
+            queue.dma_start(
+                out=out_1[n].rearrange("p m t -> p (m t)")[:, 4 * lo:4 * hi].bitcast(I32),
+                in_=y_codes[n][:, lo:hi].bitcast(I32),
+            )
+
+        def store_plane(lo, hi, queue):
+            for q in range(4):
+                queue.dma_start(
+                    out=out_2[lo:hi, 4 * q:4 * q + 4, :].rearrange("g r m -> r g m").bitcast(I32),
+                    in_=y_plane[32 * q:32 * q + 4, lo:hi, :].bitcast(I32),
+                )
+
+        nc.vector.memset(x_plane[:].bitcast(I32), 0)
+        nc.vector.memset(w1_plane[:].bitcast(I32), 0)
+        nc.vector.memset(expo_rows[:], 0.0)
+        z0 = load_z(0, 2)
+        z0[0]()
+        make_identity(nc, ident[:])
+        nc.sync.dma_start(out=x_first[:].bitcast(I32), in_=x_view[:, :, 0:8 * P].bitcast(I32))
+        nc.sync.dma_start(out=w1_half[0][:].bitcast(I32), in_=w1_view[:, :, 0:F].bitcast(I32))
+        load_plane(nc.sync, x_plane, x_scales)
+        load_plane(nc.sync, w1_plane, w1_scales)
+        nc.sync.dma_start(out=w1_half[1][:].bitcast(I32), in_=w1_view[:, :, F:2 * F].bitcast(I32))
+        z0[1]()
+        load_z(1)[0]()
+        load_w2(w2_first[0], 0, 0, G)
+        nc.sync.dma_start(out=x_rest[:].bitcast(I32), in_=x_view[:, :, 8 * P:4 * M].bitcast(I32))
+        for g in range(1, FG):
+            load_z(g + 1)[0]()
+            load_w2(w2_first[g], g, 0, G)
+        load_z(5)[0]()
+        nc.sync.dma_start(out=expo_rows[0:MT, :], in_=exposure.rearrange("(i p) -> i p", p=P))
+
+        sigmoid(0)
+        for g in range(FG):
+            stage1_mm(0, g)
+
+        steps2 = NG * MT
+        groups = [(i, i + 1) for i in range(0, steps2 - 2, 2)] + [(steps2 - 2,), (steps2 - 1,)]
+        chunk_at = {W2_PLAN[c][0]: c for c in range(NG * FG)}
+        rest_loads = [("w", 0), ("l", 0), ("l", 1), ("w", 1), ("l", 2), ("l", 3), ("w", 2), ("l", 4), ("l", 5), ("w", 3)]
+
+        def w2_step(s):
+            if s in chunk_at:
+                w2_vector(chunk_at[s])
+            if s - 1 in chunk_at:
+                w2_quant(chunk_at[s - 1])
+
+        for m in range(MT):
+            if m in chunk_at:
+                w2_alloc(chunk_at[m])
+                w2_gpsimd(chunk_at[m])
+            if m + 1 < MT:
+                sigmoid(m + 1)
+            else:
+                curvature(0)
+                curvature(1)
+            for kind, j in rest_loads[2 * m:2 * m + 2]:
+                if kind == "w":
+                    load_w2(w2_rest[j], j, G, N)
+                else:
+                    load_lr(j)
+            if m >= 1:
+                h_turn(m - 1)
+            if m == 3:
+                nc.vector.tensor_copy(out=expo_rows32[:], in_=expo_rows[:])
+                expo_bank = turn([expo_rows32[:]])
+                nc.scalar.copy(out=expo[:], in_=expo_bank[:, 0:8])
+            if m >= 1:
+                h_unturn(m - 1)
+            for g in range(FG):
+                stage1_mult(m, g)
+                if m + 1 < MT:
+                    stage1_mm(m + 1, g)
+            if m in chunk_at:
+                w2_scalar(chunk_at[m])
+            w2_step(m)
+            if m >= 1:
+                h_quant(m - 1)
+
+        stage2_mm(0)
+        h_turn(MT - 1)
+        h_unturn(MT - 1)
+        for i in range(steps2 + 4):
+            s = MT + i
+            if s in chunk_at:
+                w2_alloc(chunk_at[s])
+                w2_gpsimd(chunk_at[s])
+            if i + 2 < steps2:
+                curvature(i + 2)
+            if i + 1 < steps2:
+                stage2_mm(i + 1)
+            if i < steps2:
+                stage2_mult(i)
+            if i == 0:
+                h_quant(MT - 1)
+            if s in chunk_at:
+                w2_scalar(chunk_at[s])
+            if 0 <= i - 1 < steps2:
+                y_round(i - 1)
+            w2_step(s)
+            for group in groups:
+                if group[-1] == i - 3:
+                    y_quant(group)
+                    n, m = divmod(group[-1], MT)
+                    if n < NG - 1 and m == MT - 1:
+                        store_codes(n, 0, M, nc.sync)
+                        if n == NG - 2:
+                            store_plane(0, NG - 1, nc.sync)
+                    if n == NG - 1 and m == MT - 2:
+                        store_codes(n, 0, M - P, nc.sync)
+                    if n == NG - 1 and m == MT - 1:
+                        store_codes(n, M - P, M, nc.sync)
+                        store_plane(NG - 1, NG, nc.scalar)
+            for group in groups:
+                if group[-1] == i - 2:
+                    y_turn(group)
+                    y_unturn(group)

@@ -23,8 +23,11 @@ DG = D // G
 FG = F // G
 NG = N // G
 
-W2_PLAN = [(1, 160, 0), (2, 160, 0), (3, 160, 0), (4, 160, 0), (5, 224, 0), (6, 224, 0), (8, 224, 0), (9, 224, 0), (10, 288, 0), (12, 288, 0), (13, 288, 0), (15, 288, 0)]
-CAST = "v" * 18
+G1, S1 = 416, 0
+T2, S2 = 616, 256
+CAST = "gggggvvvvv"
+H_LAG = 2
+HEADC = 1
 IL4 = True
 
 
@@ -40,15 +43,15 @@ def tile_curvature_scaled_tangents_h2_kernel(
 
         x_plane = keep.tile([P, DG, M], U8, align_bytes=64)
         w1_plane = keep.tile([P, DG, F], U8, align_bytes=64)
-        x_first = keep.tile([P, DG, 2 * P], U32, align_bytes=64)
-        x_rest = keep.tile([P, DG, M - 2 * P], U32, align_bytes=64)
+        x_first = keep.tile([P, DG, P], U32, align_bytes=64)
+        x_mid = keep.tile([P, DG, 2 * P], U32, align_bytes=64)
+        x_rest = keep.tile([P, DG, M - 3 * P], U32, align_bytes=64)
         w1_half = [keep.tile([P, DG, F], U8, align_bytes=64, name="w1_half%d" % h) for h in range(2)]
         ident = keep.tile([P, P], F32, align_bytes=64)
         expo_rows = keep.tile([P, P], BF16, align_bytes=64)
         expo_rows32 = keep.tile([P, P], F32, align_bytes=64)
         expo = keep.tile([P, 8], F32, align_bytes=64)
-        w2_first = [keep.tile([P, 4, G], BF16, align_bytes=64, name="w2_first%d" % g) for g in range(FG)]
-        w2_rest = [keep.tile([P, 4, N - G], BF16, align_bytes=64, name="w2_rest%d" % g) for g in range(FG)]
+        w2_raw = {}
         w2_codes = [keep.tile([P, G], U32, align_bytes=64, name="w2_codes%d" % c) for c in range(NG * FG)]
         w2_plane = [keep.tile([P, G], U8, align_bytes=64, name="w2_plane%d" % c) for c in range(NG * FG)]
         h_codes = [keep.tile([P, FG * P], U32, align_bytes=64, name="h_codes%d" % m) for m in range(MT)]
@@ -63,19 +66,26 @@ def tile_curvature_scaled_tangents_h2_kernel(
         w1_view = w1_words.rearrange("g p b -> p g b")
 
         def load_z(m, halves=1):
-            rows[m] = flow.tile([P, F], BF16, tag="rows", bufs=MT, align_bytes=64, name="z%d" % m)
+            rows[m] = flow.tile([P, F], BF16, tag="rows", bufs=9, align_bytes=64, name="z%d" % m)
             w = F // halves
             return [
                 (lambda h=h: nc.sync.dma_start(out=rows[m][:, h * w:(h + 1) * w], in_=z[m * P:(m + 1) * P, h * w:(h + 1) * w]))
                 for h in range(halves)
             ]
 
-        def load_lr(m):
-            lrs[m] = flow.tile([P, N], BF16, tag="rows", bufs=MT, align_bytes=64, name="lr%d" % m)
-            nc.sync.dma_start(out=lrs[m][:], in_=log_rate[m * P:(m + 1) * P, :])
+        def load_lr(j):
+            n, m = divmod(2 * j, MT)
+            lrs[j] = flow.tile([P, 2, G], BF16, tag="rows", bufs=9, align_bytes=64, name="lr%d" % j)
+            nc.sync.dma_start(
+                out=lrs[j][:], in_=log_rate[m * P:(m + 2) * P, n * G:(n + 1) * G].rearrange("(a m) n -> m a n", a=2)
+            )
 
-        def load_w2(tile, g, lo, hi):
-            nc.sync.dma_start(out=tile[:], in_=w2[g * G:(g + 1) * G, lo:hi].rearrange("(p j) n -> p j n", j=4))
+        def load_w2(c):
+            n, g = divmod(c, FG)
+            w2_raw[c] = flow.tile([P, 4, G], BF16, tag="w2_raw", bufs=8, align_bytes=64, name="w2_raw%d" % c)
+            nc.sync.dma_start(
+                out=w2_raw[c][:], in_=w2[g * G:(g + 1) * G, n * G:(n + 1) * G].rearrange("(p j) n -> p j n", j=4)
+            )
 
         def load_plane(queue, plane, scales):
             for q in range(4):
@@ -94,14 +104,15 @@ def tile_curvature_scaled_tangents_h2_kernel(
                 )
 
         def stage1_mm(m, g):
-            xt, lo = (x_first, m * P) if m < 2 else (x_rest, (m - 2) * P)
+            xt, lo = (x_first, 0) if m == 0 else (x_mid, (m - 1) * P) if m < 3 else (x_rest, (m - 3) * P)
+            wt, wlo = w1_half[g // 2], (g % 2) * 2 * G
             acc[m, g] = psum.tile([P, G], F32, tag="acc", bufs=5, name="acc")
             for d in range(DG):
                 nc.tensor.matmul_mx(
                     out=acc[m, g][:],
                     lhsT=xt[:, d, lo:lo + P].bitcast(FP8X4),
                     lhsT_scale=x_plane[:, d, m * P:(m + 1) * P],
-                    rhs=w1_half[g // 2][:, d, (g % 2) * 2 * G:(g % 2 + 1) * 2 * G].bitcast(FP4X4),
+                    rhs=wt[:, d, wlo:wlo + 2 * G].bitcast(FP4X4),
                     rhs_scale=w1_plane[:, d, g * G:(g + 1) * G],
                     start=(d == 0),
                     stop=(d == DG - 1),
@@ -135,7 +146,7 @@ def tile_curvature_scaled_tangents_h2_kernel(
             h_tr[m] = [turn([words[:, (4 * b + s) * P:(4 * b + s + 1) * P] for s in range(4)]) for b in range(2)]
 
         def h_unturn(m):
-            h_t[m] = flow.tile([P, F // 2], F32, tag="h_t", bufs=2, align_bytes=64, name="h_t")
+            h_t[m] = flow.tile([P, F // 2], F32, tag="h_t", bufs=3, align_bytes=64, name="h_t")
             for b in range(2):
                 unturn(h_t[m][:, b * G:(b + 1) * G], h_tr[m][b], 4)
 
@@ -143,39 +154,33 @@ def tile_curvature_scaled_tangents_h2_kernel(
             nc.vector.quantize_mx(out=h_codes[m][:].bitcast(FP8X4), scales=h_plane[m][:], in_=h_t[m][:].bitcast(BF16))
 
         def w2_views(c, lo, hi):
-            n, g = divmod(c, FG)
-            src = w2_first[g][:, :, lo:hi] if n == 0 else w2_rest[g][:, :, (n - 1) * G + lo:(n - 1) * G + hi]
+            src = w2_raw[c][:, :, lo:hi]
             dst = w2_il[c][:, 4 * lo:4 * hi]
             if IL4:
                 return dst.rearrange("p (c i t) -> p c t i", i=4, t=4), src.rearrange("p t (c i) -> p c t i", i=4)
             return dst.rearrange("p (c t) -> p c t", t=4), src.rearrange("p t c -> p c t")
 
-        def w2_alloc(c):
-            w2_il[c] = flow.tile([P, 4 * G], BF16, tag="w2_il", bufs=3, align_bytes=64, name="w2_il")
-
-        def w2_vector(c):
-            lo = W2_PLAN[c][1] + W2_PLAN[c][2]
-            if lo < G:
-                dst, src = w2_views(c, lo, G)
-                nc.vector.tensor_copy(out=dst, in_=src)
-
-        def w2_scalar(c):
-            if W2_PLAN[c][1] > 0:
-                dst, src = w2_views(c, 0, W2_PLAN[c][1])
-                nc.scalar.copy(out=dst, in_=src)
-
-        def w2_gpsimd(c):
-            if W2_PLAN[c][2] > 0:
-                dst, src = w2_views(c, W2_PLAN[c][1], W2_PLAN[c][1] + W2_PLAN[c][2])
-                nc.gpsimd.tensor_scalar(out=dst, in0=src, scalar1=1.0, scalar2=-0.0, op0=ALU.mult, op1=ALU.add)
+        def w2_interleave(lo, hi, engine):
+            while lo < hi:
+                c = lo // G
+                end = min(hi, (c + 1) * G)
+                if c not in w2_il:
+                    w2_il[c] = flow.tile([P, 4 * G], BF16, tag="w2_il", bufs=3, align_bytes=64, name="w2_il")
+                dst, src = w2_views(c, lo - c * G, end - c * G)
+                if engine == "v":
+                    nc.vector.tensor_copy(out=dst, in_=src)
+                elif engine == "s":
+                    nc.scalar.copy(out=dst, in_=src)
+                else:
+                    nc.gpsimd.tensor_scalar(out=dst, in0=src, scalar1=1.0, scalar2=-0.0, op0=ALU.mult, op1=ALU.add)
+                lo = end
 
         def w2_quant(c):
             nc.vector.quantize_mx(out=w2_codes[c][:].bitcast(FP8X4), scales=w2_plane[c][:], in_=w2_il[c][:])
 
-        def curvature(i):
-            n, m = divmod(i, MT)
-            curv[i] = flow.tile([P, G], F32, tag="curv", bufs=4, align_bytes=64, name="curv")
-            nc.scalar.activation(out=curv[i][:], in_=lrs[m][:, n * G:(n + 1) * G], func=ACT.Exp)
+        def curvature(j):
+            curv[j] = flow.tile([P, 2 * G], F32, tag="curv", bufs=3, align_bytes=64, name="curv")
+            nc.scalar.activation(out=curv[j][:], in_=lrs[j][:].rearrange("m a n -> m (a n)"), func=ACT.Exp)
 
         def stage2_mm(i):
             n, m = divmod(i, MT)
@@ -191,31 +196,36 @@ def tile_curvature_scaled_tangents_h2_kernel(
                     stop=(g == FG - 1),
                 )
 
-        def stage2_mult(i):
-            n, m = divmod(i, MT)
-            y32[i] = flow.tile([P, G], F32, tag="y32", bufs=6, align_bytes=64, name="y32")
-            nc.vector.scalar_tensor_tensor(
-                out=y32[i][:], in0=acc[i][:], scalar=expo[:, m:m + 1], in1=curv[i][:], op0=ALU.mult, op1=ALU.mult
+        def stage2_mult(group):
+            k = len(group)
+            n, m = divmod(group[0], MT)
+            y32[group] = flow.tile([P, k * G], F32, tag="y32", bufs=4, align_bytes=64, name="y32")
+            for a, i in enumerate(group):
+                nc.vector.scalar_tensor_tensor(
+                    out=y32[group][:, a * G:(a + 1) * G], in0=acc[i][:], scalar=expo[:, m + a:m + a + 1],
+                    in1=curv[i // 2][:, (i % 2) * G:(i % 2 + 1) * G], op0=ALU.mult, op1=ALU.mult,
+                )
+            nc.sync.dma_start(
+                out=out_0[m * P:(m + k) * P, n * G:(n + 1) * G].rearrange("(a m) n -> m a n", a=k),
+                in_=y32[group][:].rearrange("m (a n) -> m a n", a=k),
             )
-            nc.sync.dma_start(out=out_0[m * P:(m + 1) * P, n * G:(n + 1) * G], in_=y32[i][:])
 
-        def y_round(i):
-            y_bf[i] = flow.tile([P, G], BF16, tag="y_bf", bufs=4, align_bytes=64, name="y_bf")
-            dst = y_bf[i][:].rearrange("m (u p e) -> m u p e", u=2, e=2)
-            src = y32[i][:].rearrange("m (p u e) -> m u p e", u=2, e=2)
-            if CAST[i] == "v":
+        def y_round(group, engine):
+            k = len(group)
+            y_bf[group] = flow.tile([P, k * G], BF16, tag="y_bf", bufs=2, align_bytes=64, name="y_bf")
+            dst = y_bf[group][:].rearrange("m (u p e) -> m u p e", u=2, e=2)
+            src = y32[group][:].rearrange("m (p u e) -> m u p e", u=2, e=2)
+            if engine == "v":
                 nc.vector.tensor_copy(out=dst, in_=src)
-            elif CAST[i] == "s":
+            elif engine == "s":
                 nc.scalar.copy(out=dst, in_=src)
             else:
                 nc.gpsimd.tensor_scalar(out=dst, in0=src, scalar1=1.0, scalar2=-0.0, op0=ALU.mult, op1=ALU.add)
 
         def y_turn(group):
-            src = []
-            for i in group:
-                words = y_bf[i][:].bitcast(F32)
-                src.extend([words[:, 0:P], words[:, P:2 * P]])
-            y_tr[group] = turn(src)
+            k = len(group)
+            words = y_bf[group][:].bitcast(F32)
+            y_tr[group] = turn([words[:, (u * k + a) * P:(u * k + a + 1) * P] for a in range(k) for u in range(2)])
 
         def y_unturn(group):
             k = 2 * len(group)
@@ -246,56 +256,53 @@ def tile_curvature_scaled_tangents_h2_kernel(
         nc.vector.memset(w1_plane[:].bitcast(I32), 0)
         nc.vector.memset(expo_rows[:], 0.0)
         z0 = load_z(0, 2)
-        z0[0]()
         make_identity(nc, ident[:])
-        nc.sync.dma_start(out=x_first[:].bitcast(I32), in_=x_view[:, :, 0:8 * P].bitcast(I32))
-        nc.sync.dma_start(out=w1_half[0][:].bitcast(I32), in_=w1_view[:, :, 0:F].bitcast(I32))
         load_plane(nc.sync, x_plane, x_scales)
+        nc.sync.dma_start(out=x_first[:].bitcast(I32), in_=x_view[:, :, 0:4 * P].bitcast(I32))
+        nc.sync.dma_start(out=w1_half[0][:].bitcast(I32), in_=w1_view[:, :, 0:F].bitcast(I32))
+        z0[0]()
         load_plane(nc.sync, w1_plane, w1_scales)
         nc.sync.dma_start(out=w1_half[1][:].bitcast(I32), in_=w1_view[:, :, F:2 * F].bitcast(I32))
         z0[1]()
+        if HEADC:
+            load_w2(0)
+        nc.sync.dma_start(out=x_mid[:].bitcast(I32), in_=x_view[:, :, 4 * P:12 * P].bitcast(I32))
         load_z(1)[0]()
-        load_w2(w2_first[0], 0, 0, G)
-        nc.sync.dma_start(out=x_rest[:].bitcast(I32), in_=x_view[:, :, 8 * P:4 * M].bitcast(I32))
-        for g in range(1, FG):
-            load_z(g + 1)[0]()
-            load_w2(w2_first[g], g, 0, G)
+        load_w2(HEADC)
+        load_z(2)[0]()
+        load_w2(HEADC + 1)
+        nc.sync.dma_start(out=x_rest[:].bitcast(I32), in_=x_view[:, :, 12 * P:4 * M].bitcast(I32))
+        load_z(3)[0]()
+        load_w2(HEADC + 2)
+        load_z(4)[0]()
+        load_w2(HEADC + 3)
         load_z(5)[0]()
         nc.sync.dma_start(out=expo_rows[0:MT, :], in_=exposure.rearrange("(i p) -> i p", p=P))
+        load_w2(HEADC + 4)
+        load_lr(0)
+        for c in range(HEADC + 5, 8):
+            load_lr(c - HEADC - 4)
+            load_w2(c)
 
         sigmoid(0)
         for g in range(FG):
             stage1_mm(0, g)
 
-        steps2 = NG * MT
-        groups = [(i, i + 1) for i in range(0, steps2 - 2, 2)] + [(steps2 - 2,), (steps2 - 1,)]
-        chunk_at = {W2_PLAN[c][0]: c for c in range(NG * FG)}
-        rest_loads = [("w", 0), ("l", 0), ("l", 1), ("w", 1), ("l", 2), ("l", 3), ("w", 2), ("l", 4), ("l", 5), ("w", 3)]
-
-        def w2_step(s):
-            if s in chunk_at:
-                w2_vector(chunk_at[s])
-            if s - 1 in chunk_at:
-                w2_quant(chunk_at[s - 1])
+        tiles2 = NG * MT
+        groups = [(i, i + 1) for i in range(0, tiles2 - 2, 2)] + [(tiles2 - 2,), (tiles2 - 1,)]
+        rest_loads = [[("l", 3)], [("w", 8), ("l", 4), ("w", 9)], [("l", 5), ("w", 10)], [("w", 11), ("l", 6)], [("l", 7), ("l", 8)], []]
 
         for m in range(MT):
-            if m in chunk_at:
-                w2_alloc(chunk_at[m])
-                w2_gpsimd(chunk_at[m])
+            c = m - 1 + HEADC
+            if m >= 1:
+                w2_interleave(c * G, c * G + G1, "g")
             if m + 1 < MT:
                 sigmoid(m + 1)
             else:
                 curvature(0)
-                curvature(1)
-            for kind, j in rest_loads[2 * m:2 * m + 2]:
-                if kind == "w":
-                    load_w2(w2_rest[j], j, G, N)
-                else:
-                    load_lr(j)
             if m >= 1:
                 h_turn(m - 1)
             if m == 3:
-                nc.vector.tensor_copy(out=expo_rows32[:], in_=expo_rows[:])
                 expo_bank = turn([expo_rows32[:]])
                 nc.scalar.copy(out=expo[:], in_=expo_bank[:, 0:8])
             if m >= 1:
@@ -304,47 +311,64 @@ def tile_curvature_scaled_tangents_h2_kernel(
                 stage1_mult(m, g)
                 if m + 1 < MT:
                     stage1_mm(m + 1, g)
-            if m in chunk_at:
-                w2_scalar(chunk_at[m])
-            w2_step(m)
+            if m == 0 and HEADC:
+                w2_interleave(0, G, "v")
             if m >= 1:
-                h_quant(m - 1)
+                w2_interleave(c * G + G1, c * G + G1 + S1, "s")
+                w2_interleave(c * G + G1 + S1, (c + 1) * G, "v")
+            if m == 2:
+                nc.vector.tensor_copy(out=expo_rows32[:], in_=expo_rows[:])
+            if c >= 1:
+                w2_quant(c - 1)
+            if m + 1 == MT:
+                stage2_mm(0)
+                stage2_mm(1)
+            if m >= H_LAG:
+                h_quant(m - H_LAG)
+            for kind, j in rest_loads[m]:
+                if kind == "w":
+                    load_w2(j)
+                else:
+                    load_lr(j)
 
-        stage2_mm(0)
         h_turn(MT - 1)
         h_unturn(MT - 1)
-        for i in range(steps2 + 4):
-            s = MT + i
-            if s in chunk_at:
-                w2_alloc(chunk_at[s])
-                w2_gpsimd(chunk_at[s])
-            if i + 2 < steps2:
-                curvature(i + 2)
-            if i + 1 < steps2:
-                stage2_mm(i + 1)
-            if i < steps2:
-                stage2_mult(i)
-            if i == 0:
-                h_quant(MT - 1)
-            if s in chunk_at:
-                w2_scalar(chunk_at[s])
-            if 0 <= i - 1 < steps2:
-                y_round(i - 1)
-            w2_step(s)
-            for group in groups:
-                if group[-1] == i - 3:
-                    y_quant(group)
-                    n, m = divmod(group[-1], MT)
-                    if n < NG - 1 and m == MT - 1:
-                        store_codes(n, 0, M, nc.sync)
-                        if n == NG - 2:
-                            store_plane(0, NG - 1, nc.sync)
-                    if n == NG - 1 and m == MT - 2:
-                        store_codes(n, 0, M - P, nc.sync)
-                    if n == NG - 1 and m == MT - 1:
-                        store_codes(n, M - P, M, nc.sync)
-                        store_plane(NG - 1, NG, nc.scalar)
-            for group in groups:
-                if group[-1] == i - 2:
-                    y_turn(group)
-                    y_unturn(group)
+        done, quantised = (MT - 1 + HEADC) * G, MT - 2 + HEADC
+        for j in range(len(groups) + 2):
+            if 1 <= j <= len(groups) and CAST[j - 1] == "g":
+                y_round(groups[j - 1], "g")
+            if j + 1 < tiles2 // 2:
+                curvature(j + 1)
+            if j < len(groups):
+                stage2_mult(groups[j])
+            while quantised < done // G:
+                w2_quant(quantised)
+                quantised = quantised + 1
+            if j < H_LAG:
+                h_quant(MT - H_LAG + j)
+            if j + 1 < len(groups):
+                for i in groups[j + 1]:
+                    stage2_mm(i)
+            if j < len(groups) and CAST[j] != "g":
+                y_round(groups[j], CAST[j])
+            if 1 <= j <= len(groups):
+                y_turn(groups[j - 1])
+            upto = min(done + T2, NG * FG * G)
+            w2_interleave(done, min(done + S2, upto), "s")
+            w2_interleave(min(done + S2, upto), upto, "v")
+            done = upto
+            if 1 <= j <= len(groups):
+                y_unturn(groups[j - 1])
+            if j >= 2:
+                group = groups[j - 2]
+                y_quant(group)
+                n, m = divmod(group[-1], MT)
+                if n < NG - 1 and m == MT - 1:
+                    store_codes(n, 0, M, nc.sync)
+                    if n == NG - 2:
+                        store_plane(0, NG - 1, nc.sync)
+                if n == NG - 1 and m == MT - 2:
+                    store_codes(n, 0, M - P, nc.sync)
+                if n == NG - 1 and m == MT - 1:
+                    store_codes(n, M - P, M, nc.sync)
+                    store_plane(NG - 1, NG, nc.scalar)

@@ -18,17 +18,15 @@ ALU = mybir.AluOpType
 
 P = 128
 G = 512
-MT = M // P
-DG = D // G
-FG = F // G
-NG = N // G
+M_TILES = M // P
+D_GROUPS = D // G
+F_GROUPS = F // G
+N_GROUPS = N // G
+CHUNKS = N_GROUPS * F_GROUPS
+PAIRS = N_GROUPS * M_TILES // 2
 
-G1, S1 = 416, 0
-T2, S2 = 616, 256
-CAST = "gggggvvvvv"
-H_LAG = 2
-HEADC = 1
-IL4 = True
+GPSIMD_COLUMNS = 384
+SCALAR_SIXTEENTHS = 10
 
 
 def tile_curvature_scaled_tangents_h2_kernel(
@@ -41,206 +39,209 @@ def tile_curvature_scaled_tangents_h2_kernel(
         psum = ctx.enter_context(tc.psum_pool(name="psum", bufs=1))
         ctx.enter_context(tc.manual_schedule())
 
-        x_plane = keep.tile([P, DG, M], U8, align_bytes=64)
-        w1_plane = keep.tile([P, DG, F], U8, align_bytes=64)
-        x_first = keep.tile([P, DG, P], U32, align_bytes=64)
-        x_mid = keep.tile([P, DG, 2 * P], U32, align_bytes=64)
-        x_rest = keep.tile([P, DG, M - 3 * P], U32, align_bytes=64)
-        w1_half = [keep.tile([P, DG, F], U8, align_bytes=64, name="w1_half%d" % h) for h in range(2)]
+        x_parts = [(0, 1), (1, 3), (3, M_TILES)]
+        x_codes = [keep.tile([P, D_GROUPS, (hi - lo) * P], U32, align_bytes=64, name="x_codes%d" % lo) for lo, hi in x_parts]
+        w1_codes = [keep.tile([P, D_GROUPS, F], U8, align_bytes=64, name="w1_codes%d" % h) for h in range(2)]
+        x_plane = keep.tile([P, D_GROUPS, M], U8, align_bytes=64)
+        w1_plane = keep.tile([P, D_GROUPS, F], U8, align_bytes=64)
         ident = keep.tile([P, P], F32, align_bytes=64)
         expo_rows = keep.tile([P, P], BF16, align_bytes=64)
         expo_rows32 = keep.tile([P, P], F32, align_bytes=64)
-        expo = keep.tile([P, 8], F32, align_bytes=64)
-        w2_raw = {}
-        w2_codes = [keep.tile([P, G], U32, align_bytes=64, name="w2_codes%d" % c) for c in range(NG * FG)]
-        w2_plane = [keep.tile([P, G], U8, align_bytes=64, name="w2_plane%d" % c) for c in range(NG * FG)]
-        h_codes = [keep.tile([P, FG * P], U32, align_bytes=64, name="h_codes%d" % m) for m in range(MT)]
-        h_plane = [keep.tile([P, FG * P], U8, align_bytes=64, name="h_plane%d" % m) for m in range(MT)]
-        y_codes = [keep.tile([P, M], U32, align_bytes=64, name="y_codes%d" % n) for n in range(NG)]
-        y_plane = keep.tile([P, NG, M], U8, align_bytes=64)
+        expo = keep.tile([P, M_TILES], F32, align_bytes=64)
+        w2_ring = [keep.tile([P, 4 * G], BF16, align_bytes=64, name="w2_ring%d" % k) for k in range(3)]
+        w2_codes = [keep.tile([P, G], U32, align_bytes=64, name="w2_codes%d" % c) for c in range(CHUNKS)]
+        w2_plane = [keep.tile([P, G], U8, align_bytes=64, name="w2_plane%d" % c) for c in range(CHUNKS)]
+        h_codes = [keep.tile([P, F_GROUPS * P], U32, align_bytes=64, name="h_codes%d" % m) for m in range(M_TILES)]
+        h_plane = [keep.tile([P, F_GROUPS * P], U8, align_bytes=64, name="h_plane%d" % m) for m in range(M_TILES)]
+        y_codes = [keep.tile([P, M], U32, align_bytes=64, name="y_codes%d" % n) for n in range(N_GROUPS)]
+        y_plane = keep.tile([P, N_GROUPS, M], U8, align_bytes=64)
 
-        rows, lrs, sig, acc, h_bf, h_tr, h_t, w2_il, curv, y32, y_bf, y_tr, y_t = (
-            {}, {}, {}, {}, {}, {}, {}, {}, {}, {}, {}, {}, {})
+        z_rows, rates, w2_raw, slope, curv = {}, {}, {}, {}, {}
+        u_sums, h_sorted, h_banks, h_turned = {}, {}, {}, {}
+        r_sums, y32, y_sorted, y_bank, y_turned = {}, {}, {}, {}, {}
 
-        x_view = x_words.rearrange("g p m t -> p g (m t)")
-        w1_view = w1_words.rearrange("g p b -> p g b")
+        def by_pairs(ap):
+            return ap.rearrange("m (p u e) -> m u p e", u=2, e=2)
 
-        def load_z(m, halves=1):
-            rows[m] = flow.tile([P, F], BF16, tag="rows", bufs=9, align_bytes=64, name="z%d" % m)
-            w = F // halves
-            return [
-                (lambda h=h: nc.sync.dma_start(out=rows[m][:, h * w:(h + 1) * w], in_=z[m * P:(m + 1) * P, h * w:(h + 1) * w]))
-                for h in range(halves)
-            ]
+        def as_sorted(ap):
+            return ap.rearrange("m (u p e) -> m u p e", u=2, e=2)
 
-        def load_lr(j):
-            n, m = divmod(2 * j, MT)
-            lrs[j] = flow.tile([P, 2, G], BF16, tag="rows", bufs=9, align_bytes=64, name="lr%d" % j)
-            nc.sync.dma_start(
-                out=lrs[j][:], in_=log_rate[m * P:(m + 2) * P, n * G:(n + 1) * G].rearrange("(a m) n -> m a n", a=2)
-            )
+        def load_x(part):
+            lo, hi = x_parts[part]
+            src = x_words.rearrange("g p m t -> p g (m t)")[:, :, 4 * lo * P:4 * hi * P]
+            nc.sync.dma_start(out=x_codes[part][:].bitcast(I32), in_=src.bitcast(I32))
 
-        def load_w2(c):
-            n, g = divmod(c, FG)
-            w2_raw[c] = flow.tile([P, 4, G], BF16, tag="w2_raw", bufs=8, align_bytes=64, name="w2_raw%d" % c)
-            nc.sync.dma_start(
-                out=w2_raw[c][:], in_=w2[g * G:(g + 1) * G, n * G:(n + 1) * G].rearrange("(p j) n -> p j n", j=4)
-            )
+        def load_w1(h):
+            src = w1_words.rearrange("g p b -> p g b")[:, :, h * F:(h + 1) * F]
+            nc.sync.dma_start(out=w1_codes[h][:].bitcast(I32), in_=src.bitcast(I32))
 
-        def load_plane(queue, plane, scales):
+        def load_plane(plane, scales):
             for q in range(4):
-                queue.dma_start(
+                nc.sync.dma_start(
                     out=plane[32 * q:32 * q + 4, :, :].bitcast(I32),
                     in_=scales[:, 4 * q:4 * q + 4, :].rearrange("g r n -> r g n").bitcast(I32),
                 )
 
+        def load_z(m, lo, hi):
+            if lo == 0:
+                z_rows[m] = flow.tile([P, F], BF16, tag="rows", bufs=9, align_bytes=64, name="z_rows")
+            nc.sync.dma_start(out=z_rows[m][:, lo:hi], in_=z[m * P:(m + 1) * P, lo:hi])
+
+        def load_rates(j):
+            n, m = divmod(2 * j, M_TILES)
+            rates[j] = flow.tile([P, 2, G], BF16, tag="rows", bufs=9, align_bytes=64, name="rates")
+            src = log_rate[m * P:(m + 2) * P, n * G:(n + 1) * G]
+            nc.sync.dma_start(out=rates[j][:], in_=src.rearrange("(a m) n -> m a n", a=2))
+
+        def load_w2(c):
+            n, g = divmod(c, F_GROUPS)
+            w2_raw[c] = flow.tile([P, 4, G], BF16, tag="w2_raw", bufs=8, align_bytes=64, name="w2_raw")
+            src = w2[g * G:(g + 1) * G, n * G:(n + 1) * G]
+            nc.sync.dma_start(out=w2_raw[c][:], in_=src.rearrange("(p t) n -> p t n", t=4))
+
+        def w2_buffer(c):
+            return w2_ring[c % 2 if c < M_TILES else (c - M_TILES + 2) % 3]
+
+        def w2_interleave(lo, hi, engine):
+            for c in range(lo // G, (hi + G - 1) // G):
+                a, b = max(lo - c * G, 0), min(hi - c * G, G)
+                src, dst = w2_raw[c][:, :, a:b], w2_buffer(c)[:, 4 * a:4 * b]
+                if engine == "gpsimd":
+                    nc.gpsimd.tensor_scalar(
+                        out=dst.rearrange("p (c t) -> p c t", t=4), in0=src.rearrange("p t c -> p c t"),
+                        scalar1=1.0, scalar2=-0.0, op0=ALU.mult, op1=ALU.add,
+                    )
+                else:
+                    copy = nc.scalar.copy if engine == "scalar" else nc.vector.tensor_copy
+                    copy(out=dst.rearrange("p (c i t) -> p c t i", i=4, t=4), in_=src.rearrange("p t (c i) -> p c t i", i=4))
+
+        def w2_quantise(c):
+            nc.vector.quantize_mx(out=w2_codes[c][:].bitcast(FP8X4), scales=w2_plane[c][:], in_=w2_buffer(c)[:])
+
+        def turn(blocks):
+            bank = psum.tile([P, G], F32, tag="turn", bufs=3, name="turn")
+            for s, block in enumerate(blocks):
+                nc.tensor.transpose(bank[:, s * P:(s + 1) * P], block, ident[:])
+            return bank
+
+        def unturn(words, bank, count, engine):
+            copy = nc.scalar.copy if engine == "scalar" else nc.vector.tensor_copy
+            copy(
+                out=words.rearrange("p (a m u) -> p a m u", a=count, u=2),
+                in_=bank[:, 0:2 * count * P].rearrange("p (a u m) -> p a m u", a=count, u=2),
+            )
+
         def sigmoid(m):
-            for g in range(FG):
-                sig[m, g] = flow.tile([P, G], F32, tag="sig", bufs=2 * FG, align_bytes=64, name="sig")
+            for h in range(2):
+                slope[m, h] = flow.tile([P, 2 * G], F32, tag="slope", bufs=4, align_bytes=64, name="slope")
                 nc.scalar.activation(
-                    out=sig[m, g][:].rearrange("m (u p e) -> m u p e", u=2, e=2),
-                    in_=rows[m][:, g * G:(g + 1) * G].rearrange("m (p u e) -> m u p e", u=2, e=2),
-                    func=ACT.Sigmoid,
+                    out=as_sorted(slope[m, h][:]), in_=by_pairs(z_rows[m][:, 2 * h * G:2 * (h + 1) * G]), func=ACT.Sigmoid
                 )
 
-        def stage1_mm(m, g):
-            xt, lo = (x_first, 0) if m == 0 else (x_mid, (m - 1) * P) if m < 3 else (x_rest, (m - 3) * P)
-            wt, wlo = w1_half[g // 2], (g % 2) * 2 * G
-            acc[m, g] = psum.tile([P, G], F32, tag="acc", bufs=5, name="acc")
-            for d in range(DG):
+        def u_matmul(m, g):
+            part = [k for k, (lo, hi) in enumerate(x_parts) if lo <= m < hi][0]
+            col = (m - x_parts[part][0]) * P
+            u_sums[m, g] = psum.tile([P, G], F32, tag="sums", bufs=5, name="u_sums")
+            for d in range(D_GROUPS):
                 nc.tensor.matmul_mx(
-                    out=acc[m, g][:],
-                    lhsT=xt[:, d, lo:lo + P].bitcast(FP8X4),
+                    out=u_sums[m, g][:],
+                    lhsT=x_codes[part][:, d, col:col + P].bitcast(FP8X4),
                     lhsT_scale=x_plane[:, d, m * P:(m + 1) * P],
-                    rhs=wt[:, d, wlo:wlo + 2 * G].bitcast(FP4X4),
+                    rhs=w1_codes[g // 2][:, d, (g % 2) * 2 * G:(g % 2 + 1) * 2 * G].bitcast(FP4X4),
                     rhs_scale=w1_plane[:, d, g * G:(g + 1) * G],
                     start=(d == 0),
-                    stop=(d == DG - 1),
+                    stop=(d == D_GROUPS - 1),
                 )
 
-        def stage1_mult(m, g):
+        def h_product(m, g):
             if g == 0:
-                h_bf[m] = flow.tile([P, F], BF16, tag="h_bf", bufs=2, align_bytes=64, name="h_bf")
+                h_sorted[m] = flow.tile([P, F], BF16, tag="h_sorted", bufs=2, align_bytes=64, name="h_sorted")
             nc.vector.tensor_tensor(
-                out=h_bf[m][:, g * G:(g + 1) * G].rearrange("m (u p e) -> m u p e", u=2, e=2),
-                in0=acc[m, g][:].rearrange("m (p u e) -> m u p e", u=2, e=2),
-                in1=sig[m, g][:].rearrange("m (u p e) -> m u p e", u=2, e=2),
+                out=as_sorted(h_sorted[m][:, g * G:(g + 1) * G]),
+                in0=by_pairs(u_sums[m, g][:]),
+                in1=slope[m, g // 2][:].rearrange("m (u g p e) -> m g u p e", u=2, g=2, e=2)[:, g % 2],
                 op=ALU.mult,
             )
 
-        def turn(src_words):
-            bank = psum.tile([P, G], F32, tag="turn", bufs=3, name="turn")
-            k = len(src_words)
-            for s in range(k):
-                nc.tensor.transpose(bank[:, s * P:(s + 1) * P], src_words[s], ident[:])
-            return bank
-
-        def unturn(dst_words, bank, k):
-            nc.scalar.copy(
-                out=dst_words.rearrange("p (a m u) -> p a m u", a=k // 2, u=2),
-                in_=bank[:, 0:k * P].rearrange("p (a u m) -> p a m u", a=k // 2, u=2),
-            )
-
         def h_turn(m):
-            words = h_bf[m][:].bitcast(F32)
-            h_tr[m] = [turn([words[:, (4 * b + s) * P:(4 * b + s + 1) * P] for s in range(4)]) for b in range(2)]
+            words = h_sorted[m][:].bitcast(F32)
+            h_banks[m] = [turn([words[:, (4 * b + s) * P:(4 * b + s + 1) * P] for s in range(4)]) for b in range(2)]
 
-        def h_unturn(m):
-            h_t[m] = flow.tile([P, F // 2], F32, tag="h_t", bufs=3, align_bytes=64, name="h_t")
+        def h_unturn(m, engine):
+            h_turned[m] = flow.tile([P, F // 2], F32, tag="h_turned", bufs=3, align_bytes=64, name="h_turned")
             for b in range(2):
-                unturn(h_t[m][:, b * G:(b + 1) * G], h_tr[m][b], 4)
+                unturn(h_turned[m][:, b * G:(b + 1) * G], h_banks[m][b], 2, engine)
 
-        def h_quant(m):
-            nc.vector.quantize_mx(out=h_codes[m][:].bitcast(FP8X4), scales=h_plane[m][:], in_=h_t[m][:].bitcast(BF16))
-
-        def w2_views(c, lo, hi):
-            src = w2_raw[c][:, :, lo:hi]
-            dst = w2_il[c][:, 4 * lo:4 * hi]
-            if IL4:
-                return dst.rearrange("p (c i t) -> p c t i", i=4, t=4), src.rearrange("p t (c i) -> p c t i", i=4)
-            return dst.rearrange("p (c t) -> p c t", t=4), src.rearrange("p t c -> p c t")
-
-        def w2_interleave(lo, hi, engine):
-            while lo < hi:
-                c = lo // G
-                end = min(hi, (c + 1) * G)
-                if c not in w2_il:
-                    w2_il[c] = flow.tile([P, 4 * G], BF16, tag="w2_il", bufs=3, align_bytes=64, name="w2_il")
-                dst, src = w2_views(c, lo - c * G, end - c * G)
-                if engine == "v":
-                    nc.vector.tensor_copy(out=dst, in_=src)
-                elif engine == "s":
-                    nc.scalar.copy(out=dst, in_=src)
-                else:
-                    nc.gpsimd.tensor_scalar(out=dst, in0=src, scalar1=1.0, scalar2=-0.0, op0=ALU.mult, op1=ALU.add)
-                lo = end
-
-        def w2_quant(c):
-            nc.vector.quantize_mx(out=w2_codes[c][:].bitcast(FP8X4), scales=w2_plane[c][:], in_=w2_il[c][:])
+        def h_quantise(m):
+            nc.vector.quantize_mx(out=h_codes[m][:].bitcast(FP8X4), scales=h_plane[m][:], in_=h_turned[m][:].bitcast(BF16))
 
         def curvature(j):
             curv[j] = flow.tile([P, 2 * G], F32, tag="curv", bufs=3, align_bytes=64, name="curv")
-            nc.scalar.activation(out=curv[j][:], in_=lrs[j][:].rearrange("m a n -> m (a n)"), func=ACT.Exp)
+            nc.scalar.activation(out=curv[j][:], in_=rates[j][:].rearrange("m a n -> m (a n)"), func=ACT.Exp)
 
-        def stage2_mm(i):
-            n, m = divmod(i, MT)
-            acc[i] = psum.tile([P, G], F32, tag="acc", bufs=5, name="acc")
-            for g in range(FG):
+        def curv_of(i):
+            return curv[i // 2][:, (i % 2) * G:(i % 2 + 1) * G]
+
+        def r_matmul(i):
+            n, m = divmod(i, M_TILES)
+            r_sums[i] = psum.tile([P, G], F32, tag="sums", bufs=5, name="r_sums")
+            for g in range(F_GROUPS):
                 nc.tensor.matmul_mx(
-                    out=acc[i][:],
+                    out=r_sums[i][:],
                     lhsT=h_codes[m][:, g * P:(g + 1) * P].bitcast(FP8X4),
                     lhsT_scale=h_plane[m][:, g * P:(g + 1) * P],
-                    rhs=w2_codes[n * FG + g][:].bitcast(FP8X4),
-                    rhs_scale=w2_plane[n * FG + g][:],
+                    rhs=w2_codes[n * F_GROUPS + g][:].bitcast(FP8X4),
+                    rhs_scale=w2_plane[n * F_GROUPS + g][:],
                     start=(g == 0),
-                    stop=(g == FG - 1),
+                    stop=(g == F_GROUPS - 1),
                 )
 
-        def stage2_mult(group):
-            k = len(group)
-            n, m = divmod(group[0], MT)
-            y32[group] = flow.tile([P, k * G], F32, tag="y32", bufs=4, align_bytes=64, name="y32")
-            for a, i in enumerate(group):
+        def y_product(span):
+            count = len(span)
+            n, m = divmod(span[0], M_TILES)
+            y32[span] = flow.tile([P, count * G], F32, tag="y32", bufs=4, align_bytes=64, name="y32")
+            for a, i in enumerate(span):
                 nc.vector.scalar_tensor_tensor(
-                    out=y32[group][:, a * G:(a + 1) * G], in0=acc[i][:], scalar=expo[:, m + a:m + a + 1],
-                    in1=curv[i // 2][:, (i % 2) * G:(i % 2 + 1) * G], op0=ALU.mult, op1=ALU.mult,
+                    out=y32[span][:, a * G:(a + 1) * G], in0=r_sums[i][:], scalar=expo[:, m + a:m + a + 1],
+                    in1=curv_of(i), op0=ALU.mult, op1=ALU.mult,
                 )
             nc.sync.dma_start(
-                out=out_0[m * P:(m + k) * P, n * G:(n + 1) * G].rearrange("(a m) n -> m a n", a=k),
-                in_=y32[group][:].rearrange("m (a n) -> m a n", a=k),
+                out=out_0[m * P:(m + count) * P, n * G:(n + 1) * G].rearrange("(a m) n -> m a n", a=count),
+                in_=y32[span][:].rearrange("m (a n) -> m a n", a=count),
             )
 
-        def y_round(group, engine):
-            k = len(group)
-            y_bf[group] = flow.tile([P, k * G], BF16, tag="y_bf", bufs=2, align_bytes=64, name="y_bf")
-            dst = y_bf[group][:].rearrange("m (u p e) -> m u p e", u=2, e=2)
-            src = y32[group][:].rearrange("m (p u e) -> m u p e", u=2, e=2)
-            if engine == "v":
-                nc.vector.tensor_copy(out=dst, in_=src)
-            elif engine == "s":
-                nc.scalar.copy(out=dst, in_=src)
-            else:
-                nc.gpsimd.tensor_scalar(out=dst, in0=src, scalar1=1.0, scalar2=-0.0, op0=ALU.mult, op1=ALU.add)
+        def y_round(span):
+            y_sorted[span] = flow.tile([P, len(span) * G], BF16, tag="y_sorted", bufs=3, align_bytes=64, name="y_sorted")
+            nc.vector.tensor_copy(out=as_sorted(y_sorted[span][:]), in_=by_pairs(y32[span][:]))
 
-        def y_turn(group):
-            k = len(group)
-            words = y_bf[group][:].bitcast(F32)
-            y_tr[group] = turn([words[:, (u * k + a) * P:(u * k + a + 1) * P] for a in range(k) for u in range(2)])
+        def y_round_from_psum(i):
+            m = i % M_TILES
+            y_sorted[(i,)] = flow.tile([P, G], BF16, tag="y_sorted", bufs=3, align_bytes=64, name="y_sorted")
+            for u in range(2):
+                nc.vector.scalar_tensor_tensor(
+                    out=as_sorted(y_sorted[(i,)][:])[:, u], in0=by_pairs(r_sums[i][:])[:, u], scalar=expo[:, m:m + 1],
+                    in1=by_pairs(curv_of(i))[:, u], op0=ALU.mult, op1=ALU.mult,
+                )
 
-        def y_unturn(group):
-            k = 2 * len(group)
-            y_t[group] = flow.tile([P, k * P], F32, tag="y_t", bufs=2, align_bytes=64, name="y_t")
-            unturn(y_t[group][:], y_tr[group], k)
+        def y_turn(span):
+            count = len(span)
+            words = y_sorted[span][:].bitcast(F32)
+            y_bank[span] = turn([words[:, (u * count + a) * P:(u * count + a + 1) * P] for a in range(count) for u in range(2)])
 
-        def y_quant(group):
-            n, m = divmod(group[0], MT)
-            cols = slice(m * P, (m + len(group)) * P)
+        def y_unturn(span):
+            count = len(span)
+            y_turned[span] = flow.tile([P, 2 * count * P], F32, tag="y_turned", bufs=4, align_bytes=64, name="y_turned")
+            unturn(y_turned[span][:], y_bank[span], count, "scalar")
+
+        def y_quantise(span):
+            n, m = divmod(span[0], M_TILES)
+            cols = slice(m * P, (m + len(span)) * P)
             nc.vector.quantize_mx(
-                out=y_codes[n][:, cols].bitcast(FP8X4), scales=y_plane[:, n, cols], in_=y_t[group][:].bitcast(BF16)
+                out=y_codes[n][:, cols].bitcast(FP8X4), scales=y_plane[:, n, cols], in_=y_turned[span][:].bitcast(BF16)
             )
 
-        def store_codes(n, lo, hi, queue):
-            queue.dma_start(
+        def store_codes(n, lo, hi):
+            nc.sync.dma_start(
                 out=out_1[n].rearrange("p m t -> p (m t)")[:, 4 * lo:4 * hi].bitcast(I32),
                 in_=y_codes[n][:, lo:hi].bitcast(I32),
             )
@@ -254,121 +255,125 @@ def tile_curvature_scaled_tangents_h2_kernel(
 
         nc.vector.memset(x_plane[:].bitcast(I32), 0)
         nc.vector.memset(w1_plane[:].bitcast(I32), 0)
-        nc.vector.memset(expo_rows[:], 0.0)
-        z0 = load_z(0, 2)
         make_identity(nc, ident[:])
-        load_plane(nc.sync, x_plane, x_scales)
-        nc.sync.dma_start(out=x_first[:].bitcast(I32), in_=x_view[:, :, 0:4 * P].bitcast(I32))
-        nc.sync.dma_start(out=w1_half[0][:].bitcast(I32), in_=w1_view[:, :, 0:F].bitcast(I32))
-        z0[0]()
-        load_plane(nc.sync, w1_plane, w1_scales)
-        nc.sync.dma_start(out=w1_half[1][:].bitcast(I32), in_=w1_view[:, :, F:2 * F].bitcast(I32))
-        z0[1]()
-        if HEADC:
-            load_w2(0)
-        nc.sync.dma_start(out=x_mid[:].bitcast(I32), in_=x_view[:, :, 4 * P:12 * P].bitcast(I32))
-        load_z(1)[0]()
-        load_w2(HEADC)
-        load_z(2)[0]()
-        load_w2(HEADC + 1)
-        nc.sync.dma_start(out=x_rest[:].bitcast(I32), in_=x_view[:, :, 12 * P:4 * M].bitcast(I32))
-        load_z(3)[0]()
-        load_w2(HEADC + 2)
-        load_z(4)[0]()
-        load_w2(HEADC + 3)
-        load_z(5)[0]()
-        nc.sync.dma_start(out=expo_rows[0:MT, :], in_=exposure.rearrange("(i p) -> i p", p=P))
-        load_w2(HEADC + 4)
-        load_lr(0)
-        for c in range(HEADC + 5, 8):
-            load_lr(c - HEADC - 4)
-            load_w2(c)
+        load_w2(0)
+        load_plane(x_plane, x_scales)
+        load_x(0)
+        load_w1(0)
+        load_z(0, 0, F // 2)
+        load_plane(w1_plane, w1_scales)
+        load_w1(1)
+        load_z(0, F // 2, F)
+        load_x(1)
+        w2_interleave(0, G, "vector")
+        nc.vector.memset(expo_rows[:], 0.0)
+        w2_quantise(0)
+        for m in range(1, M_TILES):
+            if m == x_parts[2][0]:
+                load_x(2)
+                nc.sync.dma_start(out=expo_rows[0:M_TILES, :], in_=exposure.rearrange("(i p) -> i p", p=P))
+            load_z(m, 0, F)
+            load_w2(m)
+        load_rates(0)
+        load_rates(1)
+        load_w2(6)
+        load_rates(2)
+        load_w2(7)
 
         sigmoid(0)
-        for g in range(FG):
-            stage1_mm(0, g)
+        for g in range(F_GROUPS):
+            u_matmul(0, g)
 
-        tiles2 = NG * MT
-        groups = [(i, i + 1) for i in range(0, tiles2 - 2, 2)] + [(tiles2 - 2,), (tiles2 - 1,)]
-        rest_loads = [[("l", 3)], [("w", 8), ("l", 4), ("w", 9)], [("l", 5), ("w", 10)], [("w", 11), ("l", 6)], [("l", 7), ("l", 8)], []]
-
-        for m in range(MT):
-            c = m - 1 + HEADC
+        last = M_TILES - 1
+        for m in range(M_TILES):
+            first_share = G if m == last else GPSIMD_COLUMNS
+            second_share = (first_share + G) // 2
             if m >= 1:
-                w2_interleave(c * G, c * G + G1, "g")
-            if m + 1 < MT:
+                w2_interleave(m * G, m * G + first_share, "gpsimd")
+            if m < last:
                 sigmoid(m + 1)
             else:
                 curvature(0)
             if m >= 1:
                 h_turn(m - 1)
-            if m == 3:
+            if m == last - 1:
                 expo_bank = turn([expo_rows32[:]])
-                nc.scalar.copy(out=expo[:], in_=expo_bank[:, 0:8])
-            if m >= 1:
-                h_unturn(m - 1)
-            for g in range(FG):
-                stage1_mult(m, g)
-                if m + 1 < MT:
-                    stage1_mm(m + 1, g)
-            if m == 0 and HEADC:
-                w2_interleave(0, G, "v")
-            if m >= 1:
-                w2_interleave(c * G + G1, c * G + G1 + S1, "s")
-                w2_interleave(c * G + G1 + S1, (c + 1) * G, "v")
-            if m == 2:
+                nc.scalar.copy(out=expo[:], in_=expo_bank[:, 0:M_TILES])
+            if 1 <= m < last:
+                h_unturn(m - 1, "scalar")
+            for g in range(F_GROUPS):
+                h_product(m, g)
+                if m < last:
+                    u_matmul(m + 1, g)
+            if m == last:
+                h_unturn(m - 1, "vector")
+                r_matmul(0)
+                r_matmul(1)
+            if 1 <= m < last:
+                w2_interleave(m * G + first_share, m * G + second_share, "scalar")
+                w2_interleave(m * G + second_share, (m + 1) * G, "vector")
+            if m == last - 2:
                 nc.vector.tensor_copy(out=expo_rows32[:], in_=expo_rows[:])
-            if c >= 1:
-                w2_quant(c - 1)
-            if m + 1 == MT:
-                stage2_mm(0)
-                stage2_mm(1)
-            if m >= H_LAG:
-                h_quant(m - H_LAG)
-            for kind, j in rest_loads[m]:
-                if kind == "w":
-                    load_w2(j)
-                else:
-                    load_lr(j)
+            if m >= 2:
+                h_quantise(m - 2)
+                w2_quantise(m - 1)
+            if m < last:
+                load_rates(m + 3)
+            if m < F_GROUPS:
+                load_w2(m + 8)
+        load_rates(PAIRS - 1)
+        h_turn(last)
+        h_unturn(last, "scalar")
 
-        h_turn(MT - 1)
-        h_unturn(MT - 1)
-        done, quantised = (MT - 1 + HEADC) * G, MT - 2 + HEADC
-        for j in range(len(groups) + 2):
-            if 1 <= j <= len(groups) and CAST[j - 1] == "g":
-                y_round(groups[j - 1], "g")
-            if j + 1 < tiles2 // 2:
-                curvature(j + 1)
-            if j < len(groups):
-                stage2_mult(groups[j])
-            while quantised < done // G:
-                w2_quant(quantised)
-                quantised = quantised + 1
-            if j < H_LAG:
-                h_quant(MT - H_LAG + j)
-            if j + 1 < len(groups):
-                for i in groups[j + 1]:
-                    stage2_mm(i)
-            if j < len(groups) and CAST[j] != "g":
-                y_round(groups[j], CAST[j])
-            if 1 <= j <= len(groups):
-                y_turn(groups[j - 1])
-            upto = min(done + T2, NG * FG * G)
-            w2_interleave(done, min(done + S2, upto), "s")
-            w2_interleave(min(done + S2, upto), upto, "v")
-            done = upto
-            if 1 <= j <= len(groups):
-                y_unturn(groups[j - 1])
+        pairs = [(2 * j, 2 * j + 1) for j in range(PAIRS)]
+        interleaved, quantised = M_TILES * G, M_TILES - 1
+        for j in range(PAIRS - 1):
+            upto = min(interleaved + (G if j < 2 else 3 * G // 2), CHUNKS * G)
+            split = interleaved + (upto - interleaved) * SCALAR_SIXTEENTHS // 16
+            if j >= 1:
+                y_turn(pairs[j - 1])
+            if j == 0:
+                curvature(1)
+            w2_interleave(interleaved, split, "scalar")
             if j >= 2:
-                group = groups[j - 2]
-                y_quant(group)
-                n, m = divmod(group[-1], MT)
-                if n < NG - 1 and m == MT - 1:
-                    store_codes(n, 0, M, nc.sync)
-                    if n == NG - 2:
-                        store_plane(0, NG - 1, nc.sync)
-                if n == NG - 1 and m == MT - 2:
-                    store_codes(n, 0, M - P, nc.sync)
-                if n == NG - 1 and m == MT - 1:
-                    store_codes(n, M - P, M, nc.sync)
-                    store_plane(NG - 1, NG, nc.scalar)
+                y_unturn(pairs[j - 2])
+            if j >= 1:
+                curvature(j + 1)
+            y_product(pairs[j])
+            if j < 2:
+                h_quantise(last - 1 + j)
+            w2_interleave(split, upto, "vector")
+            interleaved = upto
+            if j >= 2:
+                y_quantise(pairs[j - 2])
+                n, m = divmod(pairs[j - 2][1], M_TILES)
+                if m == last:
+                    store_codes(n, 0, M)
+            y_round(pairs[j])
+            ready = interleaved // G - (1 if j == 0 else 0)
+            for c in range(quantised, ready):
+                w2_quantise(c)
+            quantised = ready
+            r_matmul(2 * j + 2)
+            r_matmul(2 * j + 3)
+
+        near, end = (2 * PAIRS - 2,), (2 * PAIRS - 1,)
+        store_plane(0, N_GROUPS - 1, nc.sync)
+        y_unturn(pairs[-3])
+        y_turn(pairs[-2])
+        y_unturn(pairs[-2])
+        y_product(near)
+        y_quantise(pairs[-3])
+        y_round(near)
+        y_round_from_psum(end[0])
+        y_product(end)
+        y_turn(near)
+        y_turn(end)
+        y_unturn(near)
+        y_unturn(end)
+        y_quantise(pairs[-2])
+        store_codes(N_GROUPS - 1, 0, M - 2 * P)
+        y_quantise(near)
+        y_quantise(end)
+        store_codes(N_GROUPS - 1, M - 2 * P, M)
+        store_plane(N_GROUPS - 1, N_GROUPS, nc.scalar)

@@ -26,6 +26,7 @@ CHUNKS = N_GROUPS * F_GROUPS
 PAIRS = N_GROUPS * M_TILES // 2
 
 GPSIMD_COLUMNS = 384
+GPSIMD_COLUMNS_LATE = 128
 SCALAR_SIXTEENTHS = 10
 
 
@@ -47,7 +48,6 @@ def tile_curvature_scaled_tangents_h2_kernel(
         ident = keep.tile([P, P], F32, align_bytes=64)
         expo_rows = keep.tile([P, P], BF16, align_bytes=64)
         expo_rows32 = keep.tile([P, P], F32, align_bytes=64)
-        expo = keep.tile([P, M_TILES], F32, align_bytes=64)
         w2_ring = [keep.tile([P, 4 * G], BF16, align_bytes=64, name="w2_ring%d" % k) for k in range(3)]
         w2_codes = [keep.tile([P, G], U32, align_bytes=64, name="w2_codes%d" % c) for c in range(CHUNKS)]
         w2_plane = [keep.tile([P, G], U8, align_bytes=64, name="w2_plane%d" % c) for c in range(CHUNKS)]
@@ -102,18 +102,16 @@ def tile_curvature_scaled_tangents_h2_kernel(
         def w2_buffer(c):
             return w2_ring[c % 2 if c < M_TILES else (c - M_TILES + 2) % 3]
 
-        def w2_interleave(lo, hi, engine):
-            for c in range(lo // G, (hi + G - 1) // G):
-                a, b = max(lo - c * G, 0), min(hi - c * G, G)
-                src, dst = w2_raw[c][:, :, a:b], w2_buffer(c)[:, 4 * a:4 * b]
-                if engine == "gpsimd":
-                    nc.gpsimd.tensor_scalar(
-                        out=dst.rearrange("p (c t) -> p c t", t=4), in0=src.rearrange("p t c -> p c t"),
-                        scalar1=1.0, scalar2=-0.0, op0=ALU.mult, op1=ALU.add,
-                    )
-                else:
-                    copy = nc.scalar.copy if engine == "scalar" else nc.vector.tensor_copy
-                    copy(out=dst.rearrange("p (c i t) -> p c t i", i=4, t=4), in_=src.rearrange("p t (c i) -> p c t i", i=4))
+        def w2_interleave(c, lo, hi, engine):
+            src, dst = w2_raw[c][:, :, lo:hi], w2_buffer(c)[:, 4 * lo:4 * hi]
+            if engine == "gpsimd":
+                nc.gpsimd.tensor_scalar(
+                    out=dst.rearrange("p (c t) -> p c t", t=4), in0=src.rearrange("p t c -> p c t"),
+                    scalar1=1.0, scalar2=-0.0, op0=ALU.mult, op1=ALU.add,
+                )
+            else:
+                copy = nc.scalar.copy if engine == "scalar" else nc.vector.tensor_copy
+                copy(out=dst.rearrange("p (c i t) -> p c t i", i=4, t=4), in_=src.rearrange("p t (c i) -> p c t i", i=4))
 
         def w2_quantise(c):
             nc.vector.quantize_mx(out=w2_codes[c][:].bitcast(FP8X4), scales=w2_plane[c][:], in_=w2_buffer(c)[:])
@@ -265,7 +263,7 @@ def tile_curvature_scaled_tangents_h2_kernel(
         load_w1(1)
         load_z(0, F // 2, F)
         load_x(1)
-        w2_interleave(0, G, "vector")
+        w2_interleave(0, 0, G, "vector")
         nc.vector.memset(expo_rows[:], 0.0)
         w2_quantise(0)
         for m in range(1, M_TILES):
@@ -277,8 +275,8 @@ def tile_curvature_scaled_tangents_h2_kernel(
         load_rates(0)
         load_rates(1)
         load_w2(6)
-        load_rates(2)
         load_w2(7)
+        load_rates(2)
 
         sigmoid(0)
         for g in range(F_GROUPS):
@@ -287,18 +285,18 @@ def tile_curvature_scaled_tangents_h2_kernel(
         last = M_TILES - 1
         for m in range(M_TILES):
             first_share = G if m == last else GPSIMD_COLUMNS
-            second_share = (first_share + G) // 2
+            second_share = G if m == 1 else (first_share + G) // 2
             if m >= 1:
-                w2_interleave(m * G, m * G + first_share, "gpsimd")
+                w2_interleave(m, 0, first_share, "gpsimd")
             if m < last:
                 sigmoid(m + 1)
             else:
                 curvature(0)
             if m >= 1:
                 h_turn(m - 1)
-            if m == last - 1:
-                expo_bank = turn([expo_rows32[:]])
-                nc.scalar.copy(out=expo[:], in_=expo_bank[:, 0:M_TILES])
+            if m == last:
+                expo = psum.tile([P, G], F32, tag="sums", bufs=5, name="expo")
+                nc.tensor.transpose(expo[:, 0:P], expo_rows32[:], ident[:])
             if 1 <= m < last:
                 h_unturn(m - 1, "scalar")
             for g in range(F_GROUPS):
@@ -310,47 +308,70 @@ def tile_curvature_scaled_tangents_h2_kernel(
                 r_matmul(0)
                 r_matmul(1)
             if 1 <= m < last:
-                w2_interleave(m * G + first_share, m * G + second_share, "scalar")
-                w2_interleave(m * G + second_share, (m + 1) * G, "vector")
+                w2_interleave(m, first_share, second_share, "scalar")
+            if 2 <= m < last:
+                w2_interleave(m, second_share, G, "vector")
             if m == last - 2:
                 nc.vector.tensor_copy(out=expo_rows32[:], in_=expo_rows[:])
             if m >= 2:
                 h_quantise(m - 2)
+            if m == last:
+                h_quantise(m - 1)
+            if m >= 2:
                 w2_quantise(m - 1)
-            if m < last:
-                load_rates(m + 3)
             if m < F_GROUPS:
                 load_w2(m + 8)
+            if m < last:
+                load_rates(m + 3)
         load_rates(PAIRS - 1)
         h_turn(last)
         h_unturn(last, "scalar")
 
         pairs = [(2 * j, 2 * j + 1) for j in range(PAIRS)]
-        interleaved, quantised = M_TILES * G, M_TILES - 1
+        helped = (7, 8, 10, 11)
+        widths = {c: G - (GPSIMD_COLUMNS_LATE if c in helped else 0) for c in range(M_TILES, CHUNKS)}
+        starts = {c: sum(widths[k] for k in range(M_TILES, c)) for c in range(M_TILES, CHUNKS + 1)}
+
+        def w2_share(lo, hi, engine):
+            for c in range(M_TILES, CHUNKS):
+                a, b = max(lo - starts[c], 0), min(hi - starts[c], widths[c])
+                if a < b:
+                    w2_interleave(c, a, b, engine)
+
+        def in_eights(columns):
+            return columns // 8 * 8
+
+        second_group, third_group = starts[2 * F_GROUPS], starts[CHUNKS]
+        ends = [in_eights(second_group * k // 2) for k in (1, 2)]
+        ends = ends + [second_group + in_eights((third_group - second_group) * k // 3) for k in (1, 2)]
+        ends = ends + [third_group] * (PAIRS - 1 - len(ends))
+        interleaved, quantised = 0, M_TILES - 1
         for j in range(PAIRS - 1):
-            upto = min(interleaved + (G if j < 2 else 3 * G // 2), CHUNKS * G)
-            split = interleaved + (upto - interleaved) * SCALAR_SIXTEENTHS // 16
+            upto = ends[j]
+            split = interleaved + in_eights((upto - interleaved) * SCALAR_SIXTEENTHS // 16)
+            if j < len(helped):
+                assert helped[j] == quantised - 1 + 3
+                w2_interleave(helped[j], widths[helped[j]], G, "gpsimd")
             if j >= 1:
                 y_turn(pairs[j - 1])
             if j == 0:
                 curvature(1)
-            w2_interleave(interleaved, split, "scalar")
+            w2_share(interleaved, split, "scalar")
             if j >= 2:
                 y_unturn(pairs[j - 2])
             if j >= 1:
                 curvature(j + 1)
             y_product(pairs[j])
-            if j < 2:
-                h_quantise(last - 1 + j)
-            w2_interleave(split, upto, "vector")
+            w2_share(split, upto, "vector")
             interleaved = upto
             if j >= 2:
                 y_quantise(pairs[j - 2])
-                n, m = divmod(pairs[j - 2][1], M_TILES)
-                if m == last:
-                    store_codes(n, 0, M)
+                n, m = divmod(pairs[j - 2][0], M_TILES)
+                store_codes(n, m * P, (m + 2) * P)
             y_round(pairs[j])
-            ready = interleaved // G - (1 if j == 0 else 0)
+            if j == 0:
+                h_quantise(last)
+            ready = max(c for c in starts if starts[c] <= interleaved)
             for c in range(quantised, ready):
                 w2_quantise(c)
             quantised = ready
@@ -364,6 +385,7 @@ def tile_curvature_scaled_tangents_h2_kernel(
         y_unturn(pairs[-2])
         y_product(near)
         y_quantise(pairs[-3])
+        store_codes(N_GROUPS - 1, 0, 2 * P)
         y_round(near)
         y_round_from_psum(end[0])
         y_product(end)
@@ -372,7 +394,7 @@ def tile_curvature_scaled_tangents_h2_kernel(
         y_unturn(near)
         y_unturn(end)
         y_quantise(pairs[-2])
-        store_codes(N_GROUPS - 1, 0, M - 2 * P)
+        store_codes(N_GROUPS - 1, 2 * P, 4 * P)
         y_quantise(near)
         y_quantise(end)
         store_codes(N_GROUPS - 1, M - 2 * P, M)

from contextlib import ExitStack

import concourse.mybir as mybir
from concourse.masks import make_identity

M, D, F, N = 768, 1024, 2048, 1536
FLOPS = 2 * M * D * F + 2 * M * F * N

F32 = mybir.dt.float32
BF16 = mybir.dt.bfloat16
I32 = mybir.dt.int32
U32 = mybir.dt.uint32
U8 = mybir.dt.uint8
FP8X4 = mybir.dt.float8_e4m3fn_x4
FP4X4 = mybir.dt.float4_e2m1fn_x4
ACT = mybir.ActivationFunctionType
ALU = mybir.AluOpType

P = 128
G = 512
M_TILES = M // P
D_GROUPS = D // G
F_GROUPS = F // G
N_GROUPS = N // G
CHUNKS = N_GROUPS * F_GROUPS
PAIRS = N_GROUPS * M_TILES // 2

GPSIMD_COLUMNS = 384
GPSIMD_COLUMNS_LATE = 128
SCALAR_SIXTEENTHS = 10


def tile_curvature_scaled_tangents_h2_kernel(
    tc, x_words, x_scales, w1_words, w1_scales, z, w2, log_rate, exposure, out_0, out_1, out_2
):
    nc = tc.nc
    with ExitStack() as ctx:
        keep = ctx.enter_context(tc.tile_pool(name="keep", bufs=1))
        flow = ctx.enter_context(tc.tile_pool(name="flow", bufs=2))
        psum = ctx.enter_context(tc.psum_pool(name="psum", bufs=1))
        ctx.enter_context(tc.manual_schedule())

        x_parts = [(0, 1), (1, 3), (3, M_TILES)]
        x_codes = [keep.tile([P, D_GROUPS, (hi - lo) * P], U32, align_bytes=64, name="x_codes%d" % lo) for lo, hi in x_parts]
        w1_codes = [keep.tile([P, D_GROUPS, F], U8, align_bytes=64, name="w1_codes%d" % h) for h in range(2)]
        x_plane = keep.tile([P, D_GROUPS, M], U8, align_bytes=64)
        w1_plane = keep.tile([P, D_GROUPS, F], U8, align_bytes=64)
        ident = keep.tile([P, P], F32, align_bytes=64)
        expo_rows = keep.tile([P, P], BF16, align_bytes=64)
        expo_rows32 = keep.tile([P, P], F32, align_bytes=64)
        w2_ring = [keep.tile([P, 4 * G], BF16, align_bytes=64, name="w2_ring%d" % k) for k in range(3)]
        w2_codes = [keep.tile([P, G], U32, align_bytes=64, name="w2_codes%d" % c) for c in range(CHUNKS)]
        w2_plane = [keep.tile([P, G], U8, align_bytes=64, name="w2_plane%d" % c) for c in range(CHUNKS)]
        h_codes = [keep.tile([P, F_GROUPS * P], U32, align_bytes=64, name="h_codes%d" % m) for m in range(M_TILES)]
        h_plane = [keep.tile([P, F_GROUPS * P], U8, align_bytes=64, name="h_plane%d" % m) for m in range(M_TILES)]
        y_codes = [keep.tile([P, M], U32, align_bytes=64, name="y_codes%d" % n) for n in range(N_GROUPS)]
        y_plane = keep.tile([P, N_GROUPS, M], U8, align_bytes=64)

        z_rows, rates, w2_raw, slope, curv = {}, {}, {}, {}, {}
        u_sums, h_sorted, h_banks, h_turned = {}, {}, {}, {}
        r_sums, y32, y_sorted, y_bank, y_turned = {}, {}, {}, {}, {}

        def by_pairs(ap):
            return ap.rearrange("m (p u e) -> m u p e", u=2, e=2)

        def as_sorted(ap):
            return ap.rearrange("m (u p e) -> m u p e", u=2, e=2)

        def load_x(part):
            lo, hi = x_parts[part]
            src = x_words.rearrange("g p m t -> p g (m t)")[:, :, 4 * lo * P:4 * hi * P]
            nc.sync.dma_start(out=x_codes[part][:].bitcast(I32), in_=src.bitcast(I32))

        def load_w1(h):
            src = w1_words.rearrange("g p b -> p g b")[:, :, h * F:(h + 1) * F]
            nc.sync.dma_start(out=w1_codes[h][:].bitcast(I32), in_=src.bitcast(I32))

        def load_plane(plane, scales):
            for q in range(4):
                nc.sync.dma_start(
                    out=plane[32 * q:32 * q + 4, :, :].bitcast(I32),
                    in_=scales[:, 4 * q:4 * q + 4, :].rearrange("g r n -> r g n").bitcast(I32),
                )

        def load_z(m, lo, hi):
            if lo == 0:
                z_rows[m] = flow.tile([P, F], BF16, tag="rows", bufs=9, align_bytes=64, name="z_rows")
            nc.sync.dma_start(out=z_rows[m][:, lo:hi], in_=z[m * P:(m + 1) * P, lo:hi])

        def load_rates(j):
            n, m = divmod(2 * j, M_TILES)
            rates[j] = flow.tile([P, 2, G], BF16, tag="rows", bufs=9, align_bytes=64, name="rates")
            src = log_rate[m * P:(m + 2) * P, n * G:(n + 1) * G]
            nc.sync.dma_start(out=rates[j][:], in_=src.rearrange("(a m) n -> m a n", a=2))

        def load_w2(c):
            n, g = divmod(c, F_GROUPS)
            w2_raw[c] = flow.tile([P, 4, G], BF16, tag="w2_raw", bufs=8, align_bytes=64, name="w2_raw")
            src = w2[g * G:(g + 1) * G, n * G:(n + 1) * G]
            nc.sync.dma_start(out=w2_raw[c][:], in_=src.rearrange("(p t) n -> p t n", t=4))

        def w2_buffer(c):
            return w2_ring[c % 2 if c < M_TILES else (c - M_TILES + 2) % 3]

        def w2_interleave(c, lo, hi, engine):
            src, dst = w2_raw[c][:, :, lo:hi], w2_buffer(c)[:, 4 * lo:4 * hi]
            if engine == "gpsimd":
                nc.gpsimd.tensor_scalar(
                    out=dst.rearrange("p (c t) -> p c t", t=4), in0=src.rearrange("p t c -> p c t"),
                    scalar1=1.0, scalar2=-0.0, op0=ALU.mult, op1=ALU.add,
                )
            else:
                copy = nc.scalar.copy if engine == "scalar" else nc.vector.tensor_copy
                copy(out=dst.rearrange("p (c i t) -> p c t i", i=4, t=4), in_=src.rearrange("p t (c i) -> p c t i", i=4))

        def w2_quantise(c):
            nc.vector.quantize_mx(out=w2_codes[c][:].bitcast(FP8X4), scales=w2_plane[c][:], in_=w2_buffer(c)[:])

        def turn(blocks):
            bank = psum.tile([P, G], F32, tag="turn", bufs=3, name="turn")
            for s, block in enumerate(blocks):
                nc.tensor.transpose(bank[:, s * P:(s + 1) * P], block, ident[:])
            return bank

        def unturn(words, bank, count, engine):
            copy = nc.scalar.copy if engine == "scalar" else nc.vector.tensor_copy
            copy(
                out=words.rearrange("p (a m u) -> p a m u", a=count, u=2),
                in_=bank[:, 0:2 * count * P].rearrange("p (a u m) -> p a m u", a=count, u=2),
            )

        def sigmoid(m):
            for h in range(2):
                slope[m, h] = flow.tile([P, 2 * G], F32, tag="slope", bufs=4, align_bytes=64, name="slope")
                nc.scalar.activation(
                    out=as_sorted(slope[m, h][:]), in_=by_pairs(z_rows[m][:, 2 * h * G:2 * (h + 1) * G]), func=ACT.Sigmoid
                )

        def u_matmul(m, g):
            part = [k for k, (lo, hi) in enumerate(x_parts) if lo <= m < hi][0]
            col = (m - x_parts[part][0]) * P
            u_sums[m, g] = psum.tile([P, G], F32, tag="sums", bufs=5, name="u_sums")
            for d in range(D_GROUPS):
                nc.tensor.matmul_mx(
                    out=u_sums[m, g][:],
                    lhsT=x_codes[part][:, d, col:col + P].bitcast(FP8X4),
                    lhsT_scale=x_plane[:, d, m * P:(m + 1) * P],
                    rhs=w1_codes[g // 2][:, d, (g % 2) * 2 * G:(g % 2 + 1) * 2 * G].bitcast(FP4X4),
                    rhs_scale=w1_plane[:, d, g * G:(g + 1) * G],
                    start=(d == 0),
                    stop=(d == D_GROUPS - 1),
                )

        def h_product(m, g):
            if g == 0:
                h_sorted[m] = flow.tile([P, F], BF16, tag="h_sorted", bufs=2, align_bytes=64, name="h_sorted")
            nc.vector.tensor_tensor(
                out=as_sorted(h_sorted[m][:, g * G:(g + 1) * G]),
                in0=by_pairs(u_sums[m, g][:]),
                in1=slope[m, g // 2][:].rearrange("m (u g p e) -> m g u p e", u=2, g=2, e=2)[:, g % 2],
                op=ALU.mult,
            )

        def h_turn(m):
            words = h_sorted[m][:].bitcast(F32)
            h_banks[m] = [turn([words[:, (4 * b + s) * P:(4 * b + s + 1) * P] for s in range(4)]) for b in range(2)]

        def h_unturn(m, engine):
            h_turned[m] = flow.tile([P, F // 2], F32, tag="h_turned", bufs=3, align_bytes=64, name="h_turned")
            for b in range(2):
                unturn(h_turned[m][:, b * G:(b + 1) * G], h_banks[m][b], 2, engine)

        def h_quantise(m):
            nc.vector.quantize_mx(out=h_codes[m][:].bitcast(FP8X4), scales=h_plane[m][:], in_=h_turned[m][:].bitcast(BF16))

        def curvature(j):
            curv[j] = flow.tile([P, 2 * G], F32, tag="curv", bufs=3, align_bytes=64, name="curv")
            nc.scalar.activation(out=curv[j][:], in_=rates[j][:].rearrange("m a n -> m (a n)"), func=ACT.Exp)

        def curv_of(i):
            return curv[i // 2][:, (i % 2) * G:(i % 2 + 1) * G]

        def r_matmul(i):
            n, m = divmod(i, M_TILES)
            r_sums[i] = psum.tile([P, G], F32, tag="sums", bufs=5, name="r_sums")
            for g in range(F_GROUPS):
                nc.tensor.matmul_mx(
                    out=r_sums[i][:],
                    lhsT=h_codes[m][:, g * P:(g + 1) * P].bitcast(FP8X4),
                    lhsT_scale=h_plane[m][:, g * P:(g + 1) * P],
                    rhs=w2_codes[n * F_GROUPS + g][:].bitcast(FP8X4),
                    rhs_scale=w2_plane[n * F_GROUPS + g][:],
                    start=(g == 0),
                    stop=(g == F_GROUPS - 1),
                )

        def y_product(span):
            count = len(span)
            n, m = divmod(span[0], M_TILES)
            y32[span] = flow.tile([P, count * G], F32, tag="y32", bufs=4, align_bytes=64, name="y32")
            for a, i in enumerate(span):
                nc.vector.scalar_tensor_tensor(
                    out=y32[span][:, a * G:(a + 1) * G], in0=r_sums[i][:], scalar=expo[:, m + a:m + a + 1],
                    in1=curv_of(i), op0=ALU.mult, op1=ALU.mult,
                )
            nc.sync.dma_start(
                out=out_0[m * P:(m + count) * P, n * G:(n + 1) * G].rearrange("(a m) n -> m a n", a=count),
                in_=y32[span][:].rearrange("m (a n) -> m a n", a=count),
            )

        def y_round(span):
            y_sorted[span] = flow.tile([P, len(span) * G], BF16, tag="y_sorted", bufs=3, align_bytes=64, name="y_sorted")
            nc.vector.tensor_copy(out=as_sorted(y_sorted[span][:]), in_=by_pairs(y32[span][:]))

        def y_round_from_psum(i):
            m = i % M_TILES
            y_sorted[(i,)] = flow.tile([P, G], BF16, tag="y_sorted", bufs=3, align_bytes=64, name="y_sorted")
            for u in range(2):
                nc.vector.scalar_tensor_tensor(
                    out=as_sorted(y_sorted[(i,)][:])[:, u], in0=by_pairs(r_sums[i][:])[:, u], scalar=expo[:, m:m + 1],
                    in1=by_pairs(curv_of(i))[:, u], op0=ALU.mult, op1=ALU.mult,
                )

        def y_turn(span):
            count = len(span)
            words = y_sorted[span][:].bitcast(F32)
            y_bank[span] = turn([words[:, (u * count + a) * P:(u * count + a + 1) * P] for a in range(count) for u in range(2)])

        def y_unturn(span):
            count = len(span)
            y_turned[span] = flow.tile([P, 2 * count * P], F32, tag="y_turned", bufs=4, align_bytes=64, name="y_turned")
            unturn(y_turned[span][:], y_bank[span], count, "scalar")

        def y_quantise(span):
            n, m = divmod(span[0], M_TILES)
            cols = slice(m * P, (m + len(span)) * P)
            nc.vector.quantize_mx(
                out=y_codes[n][:, cols].bitcast(FP8X4), scales=y_plane[:, n, cols], in_=y_turned[span][:].bitcast(BF16)
            )

        def store_codes(n, lo, hi):
            nc.sync.dma_start(
                out=out_1[n].rearrange("p m t -> p (m t)")[:, 4 * lo:4 * hi].bitcast(I32),
                in_=y_codes[n][:, lo:hi].bitcast(I32),
            )

        def store_plane(lo, hi, queue):
            for q in range(4):
                queue.dma_start(
                    out=out_2[lo:hi, 4 * q:4 * q + 4, :].rearrange("g r m -> r g m").bitcast(I32),
                    in_=y_plane[32 * q:32 * q + 4, lo:hi, :].bitcast(I32),
                )

        nc.vector.memset(x_plane[:].bitcast(I32), 0)
        nc.vector.memset(w1_plane[:].bitcast(I32), 0)
        make_identity(nc, ident[:])
        load_w2(0)
        load_plane(x_plane, x_scales)
        load_x(0)
        load_w1(0)
        load_z(0, 0, F // 2)
        load_plane(w1_plane, w1_scales)
        load_w1(1)
        load_z(0, F // 2, F)
        load_x(1)
        w2_interleave(0, 0, G, "vector")
        nc.vector.memset(expo_rows[:], 0.0)
        w2_quantise(0)
        for m in range(1, M_TILES):
            if m == x_parts[2][0]:
                load_x(2)
                nc.sync.dma_start(out=expo_rows[0:M_TILES, :], in_=exposure.rearrange("(i p) -> i p", p=P))
            load_z(m, 0, F)
            load_w2(m)
        load_rates(0)
        load_rates(1)
        load_w2(6)
        load_w2(7)
        load_rates(2)

        sigmoid(0)
        for g in range(F_GROUPS):
            u_matmul(0, g)

        last = M_TILES - 1
        for m in range(M_TILES):
            first_share = G if m == last else GPSIMD_COLUMNS
            second_share = G if m == 1 else (first_share + G) // 2
            if m >= 1:
                w2_interleave(m, 0, first_share, "gpsimd")
            if m < last:
                sigmoid(m + 1)
            else:
                curvature(0)
            if m >= 1:
                h_turn(m - 1)
            if m == last:
                expo = psum.tile([P, G], F32, tag="sums", bufs=5, name="expo")
                nc.tensor.transpose(expo[:, 0:P], expo_rows32[:], ident[:])
            if 1 <= m < last:
                h_unturn(m - 1, "scalar")
            for g in range(F_GROUPS):
                h_product(m, g)
                if m < last:
                    u_matmul(m + 1, g)
            if m == last:
                h_unturn(m - 1, "vector")
                r_matmul(0)
                r_matmul(1)
            if 1 <= m < last:
                w2_interleave(m, first_share, second_share, "scalar")
            if 2 <= m < last:
                w2_interleave(m, second_share, G, "vector")
            if m == last - 2:
                nc.vector.tensor_copy(out=expo_rows32[:], in_=expo_rows[:])
            if m >= 2:
                h_quantise(m - 2)
            if m == last:
                h_quantise(m - 1)
            if m >= 2:
                w2_quantise(m - 1)
            if m < F_GROUPS:
                load_w2(m + 8)
            if m < last:
                load_rates(m + 3)
        load_rates(PAIRS - 1)
        h_turn(last)
        h_unturn(last, "scalar")

        pairs = [(2 * j, 2 * j + 1) for j in range(PAIRS)]
        helped = (7, 8, 10, 11)
        widths = {c: G - (GPSIMD_COLUMNS_LATE if c in helped else 0) for c in range(M_TILES, CHUNKS)}
        starts = {c: sum(widths[k] for k in range(M_TILES, c)) for c in range(M_TILES, CHUNKS + 1)}

        def w2_share(lo, hi, engine):
            for c in range(M_TILES, CHUNKS):
                a, b = max(lo - starts[c], 0), min(hi - starts[c], widths[c])
                if a < b:
                    w2_interleave(c, a, b, engine)

        def in_eights(columns):
            return columns // 8 * 8

        second_group, third_group = starts[2 * F_GROUPS], starts[CHUNKS]
        ends = [in_eights(second_group * k // 2) for k in (1, 2)]
        ends = ends + [second_group + in_eights((third_group - second_group) * k // 3) for k in (1, 2)]
        ends = ends + [third_group] * (PAIRS - 1 - len(ends))
        interleaved, quantised = 0, M_TILES - 1
        for j in range(PAIRS - 1):
            upto = ends[j]
            split = interleaved + in_eights((upto - interleaved) * SCALAR_SIXTEENTHS // 16)
            if j < len(helped):
                assert helped[j] == quantised - 1 + 3
                w2_interleave(helped[j], widths[helped[j]], G, "gpsimd")
            if j >= 1:
                y_turn(pairs[j - 1])
            if j == 0:
                curvature(1)
            w2_share(interleaved, split, "scalar")
            if j >= 2:
                y_unturn(pairs[j - 2])
            if j >= 1:
                curvature(j + 1)
            y_product(pairs[j])
            w2_share(split, upto, "vector")
            interleaved = upto
            if j >= 2:
                y_quantise(pairs[j - 2])
                n, m = divmod(pairs[j - 2][0], M_TILES)
                store_codes(n, m * P, (m + 2) * P)
            y_round(pairs[j])
            if j == 0:
                h_quantise(last)
            ready = max(c for c in starts if starts[c] <= interleaved)
            for c in range(quantised, ready):
                w2_quantise(c)
            quantised = ready
            r_matmul(2 * j + 2)
            r_matmul(2 * j + 3)

        near, end = (2 * PAIRS - 2,), (2 * PAIRS - 1,)
        store_plane(0, N_GROUPS - 1, nc.sync)
        y_unturn(pairs[-3])
        y_turn(pairs[-2])
        y_unturn(pairs[-2])
        y_product(near)
        y_quantise(pairs[-3])
        store_codes(N_GROUPS - 1, 0, 2 * P)
        y_round(near)
        y_round_from_psum(end[0])
        y_product(end)
        y_turn(near)
        y_turn(end)
        y_unturn(near)
        y_unturn(end)
        y_quantise(pairs[-2])
        store_codes(N_GROUPS - 1, 2 * P, 4 * P)
        y_quantise(near)
        y_quantise(end)
        store_codes(N_GROUPS - 1, M - 2 * P, M)
        store_plane(N_GROUPS - 1, N_GROUPS, nc.scalar)
